import numpy as np, ml_dtypes
CORES = [16,18,20,22]
N = 4
BF = ml_dtypes.bfloat16
W, C, B, VI, S = 4096, 4096, 256, 3, 4
def parts(rng):
    rt = rng.integers(0, 16, (N, 8, 16, W)); pf = rng.integers(0, W, (N, 8, 16, C))
    jc = np.argsort(rng.random((N, 8, C)), axis=-1)[..., :16 * B].reshape(N, 8, 16, B)
    return rt, pf, jc, rng.integers(0, 16, (N, 8, 16, B)), rng.integers(0, 16, (N, 8, B))
def pack(rt, pf, jc, fx, sr):
    return {"rt": np.ascontiguousarray(rt.reshape(N, 128, W)).astype(np.float32).astype(BF),
            "pk": np.ascontiguousarray((pf[..., :C // 2] + 4096 * pf[..., C // 2:]).reshape(N, 128, C // 2)).astype(np.int32),
            "jc": np.ascontiguousarray(jc.reshape(N, 128, B)).astype(np.int32),
            "fx": np.ascontiguousarray(fx.reshape(N, 128, B)).astype(np.float32).astype(BF), "sr": np.ascontiguousarray(sr).astype(np.int32)}
def setup_inputs(rng):
    return pack(*parts(rng))
def setup_inputs_ties(rng):
    rt, pf, jc, fx, sr = parts(rng)
    pool = rng.integers(0, 16, (N, 8, 16, 8)); pool[:, 1::2] = rng.integers(0, 2, (N, 4, 16, 8))
    rt = np.take_along_axis(pool, rng.integers(0, 8, (N, 8, 1, W)), 3)
    fx = np.where(rng.random((N, 8, 1, B)) < 0.5, np.take_along_axis(pool, rng.integers(0, 8, (N, 8, 1, B)), 3), fx)
    q = rng.permutation(C)[:C // 8]; pf[..., q] = pf[:, :, :1, q]
    return pack(rt, pf, jc, fx, sr)
def setup_inputs_rounds(rng):
    rt, pf, jc, fx, sr = parts(rng); h = W // 2
    o = np.argsort(rng.random((N, 8, W)), axis=-1); light = np.zeros((N, 8, W), bool); np.put_along_axis(light, o[..., :h], True, 2)
    rt = np.where(light[:, :, None, :], rng.integers(0, 2, (N, 8, 16, W)), rng.integers(8, 16, (N, 8, 16, W)))
    ln = rng.integers(1, S + 2, (8, B)); back = (rng.random((8, B)) * ln).astype(np.int64)
    ln[0] = S; back[0] = 0; ln[1] = S + 1; ln[2] = 1; back[2] = 0
    if np.count_nonzero(ln <= S) % 2 == 0:
        ln[3, 0] = S + 1 if ln[3, 0] <= S else S; back[3, 0] = 0
    s0 = rng.integers(0, 16, (8, B)); a = (np.arange(16)[None, :, None] - s0[:, None, :]) % 16
    nxt = (np.where(a == ln[:, None, :] - 1, back[:, None, :], a + 1) + s0[:, None, :]) % 16
    pc = np.argsort(rng.random((8, C)), axis=-1)[:, :16 * B]
    kap = rng.integers(0, 16, (8, C)); np.put_along_axis(kap, pc, nxt.reshape(8, 16 * B), 1)
    one = kap[None, :, None, :] == np.arange(16)[None, None, :, None]
    pf = np.take_along_axis(o[:, :, None, :], rng.integers(0, h, (N, 8, 16, C)) + np.where(one, 0, h), 3)
    e = np.argsort(rng.random((N, 8, B)), axis=-1)
    jc = np.take_along_axis(np.broadcast_to(pc.reshape(1, 8, 16, B), (N, 8, 16, B)), np.broadcast_to(e[:, :, None, :], (N, 8, 16, B)), 3)
    sr = np.take_along_axis(np.broadcast_to(s0[None], (N, 8, B)), e, 2)
    return pack(rt, pf, jc, rng.integers(0, 2, (N, 8, 16, B)), sr)
def setup_inputs_full(rng):
    h = W // 2; u = h // 2; rows = np.arange(16)
    side = (np.arange(N)[:, None] + np.arange(8)[None, :]) % 2 * h
    o = np.argsort(rng.random((N, 8, h)), axis=-1) + side[:, :, None]; light = np.zeros((N, 8, W), bool); np.put_along_axis(light, o[..., :u], True, 2)
    rt = np.where(light[:, :, None, :], rng.integers(0, 2, (N, 8, 16, W)), rng.integers(8, 16, (N, 8, 16, W)))
    s0 = 2 * rng.permutation(8) + rng.integers(0, 2, 8); a = (rows[None, :] - s0[:, None]) % 16
    nxt = (np.where(a == S - 1, 0, a + 1) + s0[:, None]) % 16
    lower = np.argsort(rng.random((8, C // 2)), axis=-1)[:, :8 * B]; upper = np.argsort(rng.random((8, C // 2)), axis=-1)[:, :8 * B] + C // 2
    pc = np.concatenate([lower, upper], axis=1).reshape(8, 16, B)
    kap = rng.integers(0, 16, (N, 8, C))
    np.put_along_axis(kap, np.broadcast_to(pc.reshape(1, 8, 16 * B), (N, 8, 16 * B)), np.broadcast_to(np.repeat(nxt, B, axis=1)[None], (N, 8, 16 * B)), 2)
    whole = int(rng.integers(0, 8))
    for g in range(8):
        if g != whole: kap[1::2, g, int(pc[g, (s0[g] + S - 1) % 16, 0])] = (s0[g] + S) % 16
    one = kap[:, :, None, :] == rows[None, None, :, None]
    pf = np.take_along_axis(o[:, :, None, :], rng.integers(0, u, (N, 8, 16, C)) + np.where(one, 0, u), 3)
    e = np.argsort(rng.random((N, 8, 16, B)), axis=-1)
    jc = np.take_along_axis(np.broadcast_to(pc[None], (N, 8, 16, B)), e, 3)
    return pack(rt, pf, jc, rng.integers(0, 2, (N, 8, 16, B)), np.broadcast_to(s0[None, :, None], (N, 8, B)))
def setup_inputs_ends(rng):
    rt, pf, jc, fx, sr = parts(rng)
    pf[:, ::2] = rng.choice(np.array([0, 1, W // 2, W - 1]), (N, 4, 16, C)); pf[:, 1::2, :, C // 2 - 1] = W - 1; pf[:, 1::2, :, C - 1] = W - 1
    jc[:, ::2] = np.concatenate([np.arange(8 * B), np.arange(C - 8 * B, C)]).reshape(16, B)
    rt[:, 1::2] = 15 * rng.integers(0, 2, (N, 4, 16, W)); fx = 15 * rng.integers(0, 2, (N, 8, 16, B)); sr = 15 * rng.integers(0, 2, (N, 8, B))
    o = rng.permutation(W); n = B // 2; hi = o[:W // 4]; mid = o[W // 4:W // 2]; lo = o[W // 2:3 * W // 4]
    rt[:, 1][:, :, hi] = 15; rt[:, 1][:, :, mid] = 14; rt[:, 1][:, :, lo] = 0
    for q in range(N):
        x = rng.permutation(B)[:n]; p = np.argsort(rng.random((16, n)), axis=0)[:3]; c = jc[q, 1, p, x]
        for i, k, a, b in ((0, p[1], mid, hi), (1, p[2], hi, lo), (2, p[1], lo, hi)):
            pf[q, 1][:, c[i]] = rng.choice(b, (16, n)); pf[q, 1][k, c[i]] = rng.choice(a, n)
        fx[q, 1][:, x] = 0; sr[q, 1][x] = p[0]
    return pack(rt, pf, jc, fx, sr)
def setup_inputs_spread(rng):
    rt, pf, jc, fx, sr = parts(rng)
    rt = np.minimum((16 * rng.random((N, 8, 16, W)) ** np.exp2(rng.integers(-2, 4, (N, 8, 1, W)))).astype(np.int64), 15)
    pf = np.minimum((W * rng.random((N, 8, 16, C)) ** np.exp2(rng.integers(-2, 4, (N, 8, 1, C)))).astype(np.int64), W - 1)
    fx = np.minimum((16 * rng.random((N, 8, 16, B)) ** np.exp2(rng.integers(-2, 4, (N, 8, 1, B)))).astype(np.int64), 15)
    sr = np.minimum((16 * rng.random((N, 8, B)) ** np.exp2(rng.integers(-1, 3, (N, 8, 1)))).astype(np.int64), 15)
    return pack(rt, pf, jc, fx, sr)
def check_inputs(d):
    bad = []
    for k in ("rt", "fx"):
        a = np.asarray(d[k]).astype(np.float32)
        if not np.all((a >= 0) & (a <= 15) & (a == np.floor(a))): bad.append("whole numbers of " + k)
    a = np.asarray(d["pk"]).astype(np.int64)
    if np.min(a) < 0 or np.max(a & 4095) >= W or np.max(a >> 12) >= W: bad.append("range of pk")
    for k, hi in (("jc", C - 1), ("sr", 15)):
        if np.min(d[k]) < 0 or np.max(d[k]) > hi: bad.append("range of " + k)
    s = np.sort(np.asarray(d["jc"]).reshape(N, 8, 16 * B), axis=-1)
    if np.any(s[..., 1:] == s[..., :-1]): bad.append("courts of a group differ")
    return bad
def reference(rt, pk, jc, fx, sr):
    R = rt.astype(np.float32).astype(np.int32).reshape(N, 8, 16, W); f = fx.astype(np.float32).astype(np.int32).reshape(N, 8, 16, B)
    two = pk.astype(np.int32).reshape(N, 8, 16, C // 2); pf = np.concatenate([two & 4095, two >> 12], axis=3)
    J = jc.astype(np.int32).reshape(N, 8, 16, B); start = sr.astype(np.int32); Z = np.zeros(N, np.int32); rows = np.arange(16, dtype=np.int32)
    for t in range(VI):
        if t > 0:
            f = np.roll(f, 1, axis=0); J = np.roll(J, 1, axis=0); start = np.roll(start, 1, axis=0)
        m = np.zeros((N, 8, 16, B), np.int32); v = np.zeros((N, 8, 16, B), np.int32); num = np.zeros((N, 8, 16, B), np.int32)
        p = start; go = np.ones((N, 8, B), bool); first = np.zeros((N, 8, B), np.int32); new = np.zeros((N, 8, B), np.int32)
        for s in range(1, S + 1):
            c = np.take_along_axis(J, p[:, :, None, :], 2)
            n = np.take_along_axis(pf, np.broadcast_to(c, (N, 8, 16, B)), 3)
            x = np.take_along_axis(R, np.broadcast_to(n.reshape(N, 8, 1, 16 * B), (N, 8, 16, 16 * B)), 3).reshape(N, 8, 16, 16, B)
            dist = np.add.reduce(np.abs(x - f[:, :, :, None, :]), axis=2)
            k = np.argmin(dist, axis=2).astype(np.int32)
            kk = k[:, :, None, :]; nk = np.take_along_axis(n, kk, 2)
            rule = np.take_along_axis(R, np.broadcast_to(nk, (N, 8, 16, B)), 3)
            here = (rows[None, None, :, None] == p[:, :, None, :]) & go[:, :, None, :]
            v = np.where(here, kk, v); num = np.where(here, nk, num); m = np.where(here, np.int32(s), m)
            f = np.where(go[:, :, None, :], np.abs(f - rule), f)
            mk = np.take_along_axis(m, kk, 2)[:, :, 0]; nr = np.take_along_axis(num, kk, 2)
            shut = go & (mk > 0)
            tot = np.add.reduce(np.take_along_axis(R, np.broadcast_to(nr, (N, 8, 16, B)), 3), axis=2)
            odd = ((tot + Z[:, None, None]) & 1) == 1
            new = np.where(shut, np.where(odd, nk[:, :, 0], nr[:, :, 0]), new); first = np.where(shut, mk, first)
            go = go & ~shut; p = np.where(go, k, p)
        closed = first > 0
        loop = closed[:, :, None, :] & (m >= first[:, :, None, :])
        at = np.broadcast_to(J.reshape(N, 8, 1, 16 * B), (N, 8, 16, 16 * B))
        old = np.take_along_axis(pf, at, 3).reshape(N, 8, 16, 16, B)
        hit = loop[:, :, None] & (v[:, :, None] == rows[None, None, :, None, None])
        np.put_along_axis(pf, at, np.where(hit, new[:, :, None, None, :], old).reshape(N, 8, 16, 16 * B), 3)
        Z = Z + np.add.reduce(closed.astype(np.int32), axis=(1, 2))
    return {"yp": (pf[..., :C // 2] + 4096 * pf[..., C // 2:]).reshape(N, 128, C // 2).astype(np.float32), "yf": f.reshape(N, 128, B).astype(np.float32).astype(BF)}

@@ -1,0 +1,352 @@
+from concourse.mybir import dt, AluOpType, AxisListType, ActivationFunctionType
+import comms_topo
+
+AO = AluOpType
+AF = ActivationFunctionType
+CH = [(0, 5), (5, 10), (10, 14), (14, 16)]
+VEXP = 2
+
+F32, BF, I32, U16 = "float32", "bfloat16", "int32", "uint16"
+SCRATCH = {}
+
+
+def _s(name, cols, dtype, where="sbuf"):
+    SCRATCH[name] = (where, [128] + (cols if isinstance(cols, list) else [cols]), dtype)
+
+
+for _n, _c, _d in [
+        ("R", 4112, BF), ("PF", 5136, F32), ("PK", 2048, I32), ("TI", 2048, I32), ("YO", 2048, F32),
+        ("JI", [16, 16], I32), ("JF", [16, 16], F32), ("JT", [16, 128], F32), ("SRI", 256, I32), ("SRB", 256, BF),
+        ("SRG", 256, BF), ("FX0", 256, BF), ("FIN1", 256, BF), ("FIN2", 256, BF),
+        ("FO0", 256, BF), ("FO1", 256, BF), ("FO2", 256, BF),
+        ("ST0", 288, F32), ("ST1", 288, F32), ("ST2", 288, F32),
+        ("FS", 4096, BF), ("FE", 4096, BF), ("D2", 4096, BF), ("A3", [16, 256], BF),
+        ("NU", 1024, U16), ("NHF", 1024, F32), ("DL", 1024, F32), ("BB", 1024, F32), ("SEL", 256, F32), ("OHD", 256, F32),
+        ("SC", 256, F32), ("KH", 80, I32), ("KK", 80, I32), ("HH", 80, F32), ("OPN", 96, F32), ("LST", 64, F32),
+        ("CC", 16, I32), ("T0", 16, F32), ("T1", 16, F32), ("T2", 16, F32), ("T3", 16, F32), ("FA", 16, I32),
+        ("FL", 16, U16), ("LU", 16, U16), ("DP", 80, I32), ("AS", 80, I32), ("OD", 80, I32), ("CLB", 80, F32),
+        ("CK", 80, F32), ("KSS", 80, F32), ("H16", 80, F32), ("EQB", 80, F32), ("GB", 80, F32), ("PG", 80, F32), ("UB", 80, F32),
+        ("QB", 480, F32), ("QS", 480, F32), ("DF", 32, F32), ("DG", 32, F32), ("RS", 32, F32), ("LJA", 16, F32), ("LJD", 16, U16), ("LKD", 16, U16),
+        ("KM", 80, F32), ("KU", 80, F32), ("LC", 64, U16), ("Q0", 64, F32), ("Q1", 64, F32), ("Q2", 64, F32), ("SL", 64, U16),
+        ("ZR", 1, F32), ("ZA", 1, F32), ("ZB", 1, F32),
+        ("IM", 160, F32), ("IG", 128, F32), ("IPI", 2, I32), ("IQI", 2, I32), ("IGI", 2, I32), ("CF", 4, F32),
+        ("IDN", 128, F32), ("WB", 144, BF), ("BO", 128, F32), ("ONE", 128, F32), ("L8", 128, BF), ("MG", 8, F32), ("E16", 16, F32),
+        ("OHW", 48, F32), ("KEEP", 1280, BF), ("RST", 256, F32), ("KEEP5", 480, F32), ("XRI", 256, I32), ("XREP", 256, U16),
+        ("IA", 16, F32), ("XL", 16, F32), ("XL16", 16, F32), ("TRI", 64, F32), ("TR", 64, F32), ("SI", 80, F32), ("PLC", 256, F32),
+        ("QK", 256, F32), ("XZ", 256, F32), ("XA", 256, F32), ("XB", 256, F32), ("XC", 256, F32)]:
+    _s(_n, _c, _d)
+for _n in ["KEY0", "KEY1", "AUX0", "AUX1", "HP0", "HP1", "HP2", "HP3"]:
+    _s(_n, 512, F32, "psum")
+
+SEMAPHORES = ["sv", "ss", "sp", "sg", "aS1", "aS2", "aF1", "aF2", "ls"] + ["d%d" % i for i in range(12)]
+
+
+def rank_program(g, core, T, topo):
+    rank = T.rank_of(core)
+    if rank is None:
+        return
+    nrank = len(T.cores)
+    ENG = {"V": (g.vector, "sv"), "S": (g.scalar, "ss"), "P": (g.tensor, "sp"), "G": (g, "sg"), "Y": (g.sync, None)}
+    cnt = {s: 0 for s in SEMAPHORES}
+    waited, Wr, Rd, ndma = {}, {}, {}, [0]
+
+    def need(e, sem, val):
+        if waited.get((e, sem), 0) < val:
+            ENG[e][0].wait_ge(T.sem[sem], val)
+            waited[(e, sem)] = val
+
+    def sync(e, reads, writes):
+        own, todo = ENG[e][1], {}
+        for k in reads:
+            for s, v in Wr.get(k, {}).items():
+                todo[s] = max(todo.get(s, 0), v)
+        for k in writes:
+            for s, v in Wr.get(k, {}).items():
+                todo[s] = max(todo.get(s, 0), v)
+            for s, v in Rd.get(k, {}).items():
+                if s != own:
+                    todo[s] = max(todo.get(s, 0), v)
+        for s, v in todo.items():
+            need(e, s, v)
+
+    def note(sem, val, reads, writes):
+        for k in reads:
+            Rd.setdefault(k, {})[sem] = val
+        for k in writes:
+            Wr.setdefault(k, {})[sem] = val
+
+    def run(e, reads, writes, name, *a, **kw):
+        reads, writes = reads.split(), writes.split()
+        sync(e, reads, writes)
+        q, sem = ENG[e]
+        ins = {"tc": lambda: q.tensor_copy(*a, **kw), "tt": lambda: q.tensor_tensor(*a, **kw), "ts": lambda: q.tensor_scalar(*a, **kw),
+               "scan": lambda: q.tensor_tensor_scan(*a, **kw), "memset": lambda: q.memset(*a, **kw), "red": lambda: q.tensor_reduce(*a, **kw),
+               "act": lambda: q.activation(*a, **kw), "mm": lambda: q.matmul(*a, **kw), "iota": lambda: q.iota(*a, **kw)}[name]()
+        cnt[sem] += 1
+        ins.then_inc(T.sem[sem], 1)
+        note(sem, cnt[sem], reads, writes)
+
+    def V(reads, writes, name, *a, **kw):
+        run("V", reads, writes, name, *a, **kw)
+
+    def S(reads, writes, out, in_, func, **kw):
+        run("S", reads, writes, "act", out, in_, func, **kw)
+
+    def mms(reads, writes, calls):
+        sync("P", reads.split(), writes.split())
+        for c in calls[:-1]:
+            g.tensor.matmul(*c)
+        run("P", reads, writes, "mm", *calls[-1])
+
+    def dma(e, reads, writes, out, in_):
+        reads, writes = reads.split(), writes.split()
+        sync(e, reads, writes)
+        sem = "d%d" % ndma[0]
+        ndma[0] += 1
+        ENG[e][0].dma_start(out, in_).then_inc(T.sem[sem], 16)
+        cnt[sem] = 16
+        note(sem, 16, reads, writes)
+
+    def send(dst_rank, src, dst, arr, key):
+        d = T.cores[dst_rank]
+        rid, pid, _ = topo.addr(d)
+        sync("G", [key], [])
+        g.remote_dma(out_ap=dst, in_ap=src, remote_sem=T.sem[arr], local_sem=T.sem["ls"], pid=pid, routing_id=rid,
+                     dma_engine_mask=topo.mask(core, d))
+        cnt["ls"] += len(topo.engines(core, d))
+
+    narr = len(topo.engines(core, T.cores[(rank + 1) % nrank]))
+
+    dma("Y", "", "JI", T.JI[:, :, :], T.jc[:])
+    dma("S", "", "SRI", T.SRI[0:8, :], T.sr[:])
+    dma("S", "", "FX0", T.FX0[:], T.fx[:])
+    dma("Y", "", "PK0", T.PK[:, 0:1024], T.pk[:, 0:1024])
+    dma("Y", "", "PK1", T.PK[:, 1024:2048], T.pk[:, 1024:2048])
+    dma("Y", "", "R", T.R[:, 0:4096], T.rt[:])
+
+    big = {"allow_small_or_imprecise_dtypes": True}
+
+    def iota(name, pat, base, cm, out=None):
+        run("G", "", name, "iota", T[name][:] if out is None else out, pat, base, cm, **({} if name in ("IPI", "XRI") else big))
+    iota("IPI", [[0, 2]], 0, 1)
+    iota("IM", [[1, 160]], 0, 0)
+    iota("IG", [[1, 8], [0, 16]], 0, 0)
+    iota("PLC", [[0, 16], [8192, 16]], -16777215, 0)
+    iota("QK", [[0, 16], [1, 16]], 0, 0)
+    iota("IA", [[16, 16]], 0, 0)
+    iota("XRI", [[16, 256]], 0, 0)
+    iota("TRI", [[256, 4], [16, 16]], 4097, 0)
+    iota("SI", [[0, 16], [256, 5]], 0, 0)
+    V("IPI", "IQI", "ts", T.IQI[:], T.IPI[:], 15, None, AO.bitwise_and)
+    V("IPI", "IGI", "ts", T.IGI[:], T.IPI[:], 4, None, AO.arith_shift_right)
+    V("IPI", "CF0", "tc", T.CF[:, 0:1], T.IPI[:, 0:1])
+    V("IQI", "CF1", "tc", T.CF[:, 1:2], T.IQI[:, 0:1])
+    V("IGI", "CF2", "tc", T.CF[:, 2:3], T.IGI[:, 0:1])
+    V("IGI", "CF3", "ts", T.CF[:, 3:4], T.IGI[:, 0:1], 16.0, 15.0, AO.mult, AO.add)
+    p_c, q_c, g_c, e_c = [T.CF[:, i:i + 1] for i in range(4)]
+    V("IG CF0", "L8", "ts", T.L8[0:8, :], T.IG[0:8, :], T.CF[0:8, 0:1], None, AO.is_equal)
+    V("IM CF3", "WB", "ts", T.WB[:, 0:143], T.IM[:, 0:143], e_c, 131072.0, AO.is_equal, AO.mult)
+    V("IM CF2", "MG", "ts", T.MG[:], T.IM[:, 0:8], g_c, None, AO.is_equal)
+    V("IM CF1", "E16", "ts", T.E16[:], T.IM[:, 0:16], q_c, None, AO.is_equal)
+    V("", "KEEP", "memset", T.KEEP[:], 1.0)
+    V("", "XZ", "memset", T.XZ[:], 0.0)
+    V("", "KEEP", "memset", T.KEEP[:, 0::16], 0.0)
+
+    V("SRI", "SRB", "tc", T.SRB[0:8, :], T.SRI[0:8, :])
+    mms("L8 SRB", "AUX0", [(T.AUX0[:, 0:256], T.L8[0:8, :], T.SRB[0:8, :], True, True)])
+    V("JI", "JF", "tc", T.JF[:, :, :], T.JI[:, :, :])
+    V("AUX0", "SRG", "tc", T.SRG[:], T.AUX0[:, 0:256])
+    mms("WB SRG", "AUX1", [(T.AUX1[:, 0:16], T.WB[:, 15 - b:143 - b], T.SRG[:, b::16], b == 0, b == 15) for b in range(16)])
+    for h in range(8):
+        V("JF MG", "JT", "ts", T.JT[:, :, 16 * h:16 * h + 16], T.JF[:, :, :], T.MG[:, h:h + 1], None, AO.mult)
+    mms("JT E16", "KEY1", [(T.KEY1[:, 16 * a:16 * a + 16], T.JT[:, a, :], T.E16[:], True, True) for a in range(16)])
+    V("AUX1", "XZ", "ts", T.XZ[:, 0::16], T.AUX1[:, 0:16], 2.0 ** -21, None, AO.mult)
+    V("AUX1", "ST0", "ts", T.ST0[:, 272:288], T.AUX1[:, 0:16], 2.0 ** -21, None, AO.mult)
+    V("KEEP XZ", "XA", "scan", T.XA[:], T.KEEP[:, 0:256], T.XZ[:], 0.0, AO.mult, AO.add)
+    V("XA QK", "XB", "tt", T.XB[:], T.XA[:], T.QK[:], AO.is_equal)
+    V("KEY1 PLC", "ST0", "tt", T.ST0[:, 0:256], T.KEY1[:, 0:256], T.PLC[:], AO.add)
+    V("KEY1 XB", "XC", "tt", T.XC[:], T.KEY1[:, 0:256], T.XB[:], AO.mult)
+    V("KEEP XC", "XA", "scan", T.XA[:], T.KEEP[:, 0:256], T.XC[:], 0.0, AO.mult, AO.add)
+    V("XA", "ST0", "ts", T.ST0[:, 256:272], T.XA[:, 15::16], 1.0, None, AO.add)
+    send((rank + 1) % nrank, T.ST0[:], T.ST1[:], "aS1", "ST0")
+    send((rank + 2) % nrank, T.ST0[:], T.ST2[:], "aS2", "ST0")
+    Wr["ST1"], Wr["ST2"] = {"aS1": narr}, {"aS2": narr}
+    Wr["FIN1"], Wr["FIN2"] = {"aF1": narr}, {"aF2": narr}
+
+    V("", "FS", "memset", T.FS[:], 0.0)
+    V("IM CF0", "IDN", "ts", T.IDN[:], T.IM[:, 0:128], p_c, None, AO.is_equal)
+    V("", "RST", "memset", T.RST[:], 0.0)
+    V("", "PFT", "memset", T.PF[:, 0:16], 4096.0)
+    V("XRI", "XREP", "tc", T.XREP[:], T.XRI[:])
+    V("", "RST", "memset", T.RST[:, 0::16], 67108864.0)
+    V("", "PFT", "memset", T.PF[:, 4080:5136], 4096.0)
+    V("", "RZ", "memset", T.R[:, 4096:4112], 0.0)
+    V("IA CF1", "XL", "ts", T.XL[:], T.IA[:], q_c, None, AO.add)
+    V("", "OPN", "memset", T.OPN[:], 1.0)
+    V("XL", "XL16", "ts", T.XL16[:], T.XL[:], 16.0, None, AO.mult)
+    V("", "KK4", "memset", T.KK[:], -16)
+
+    for q in range(4):
+        c0, c1, k = 512 * q, 512 * q + 512, str(q)
+        V("PK%d" % (q // 2), "TI" + k, "ts", T.TI[:, c0:c1], T.PK[:, c0:c1], 12, None, AO.arith_shift_right)
+        if q > 0:
+            unpack_lo(V, T, q - 1)
+        V("PFT TI" + k, "PFH" + k, "tc", T.PF[:, 2049 + c0:2049 + c1], T.TI[:, c0:c1])
+        S("PFH" + k, "HP" + k, T["HP" + k][:], T.PF[:, 2049 + c0:2049 + c1], AF.Copy, scale=4096.0)
+    unpack_lo(V, T, 3)
+    PFA = "PFT " + " ".join("PFH%d PFL%d" % (q, q) for q in range(4))
+
+    def late_constants():
+        V("IG CF2", "BO", "ts", T.BO[:], T.IG[:], g_c, None, AO.is_equal)
+        V("", "ONE", "memset", T.ONE[:], 1.0)
+        V("IM CF1", "OHW", "ts", T.OHW[:, 0:16], T.IM[:, 0:16], q_c, None, AO.is_equal)
+        V("IM CF1", "OHW", "ts", T.OHW[:, 16:32], T.IM[:, 0:16], q_c, None, AO.is_equal)
+        V("", "OHW", "memset", T.OHW[:, 32:48], 0.0)
+        V("", "KEEP5", "memset", T.KEEP5[:], 1.0)
+        V("TRI CF1", "TR", "ts", T.TR[:], T.TRI[:], q_c, None, AO.add)
+        V("", "SI", "memset", T.SI[:, 4::5], 0.0)
+        V("", "KEEP5", "memset", T.KEEP5[:, 0::5], 0.0)
+        V("", "AS", "memset", T.AS[:], 0)
+        V("", "EQB", "memset", T.EQB[:], 0.0)
+        V("", "HH", "memset", T.HH[:, 4::5], 0.0)
+
+    nstep = 0
+    for t in range(3):
+        st = T["ST%d" % t]
+        stk = "ST%d" % t
+        fin, fk = (T.FX0, "FX0") if t == 0 else (T["FIN%d" % t], "FIN%d" % t)
+        fo, fok = T["FO%d" % t], "FO%d" % t
+        V(stk, "LST1", "tc", T.LST[:, 0:16], st[:, 256:272])
+        V(stk, "LU", "tc", T.LU[:], st[:, 256:272])
+        V(stk, "HH1", "tc", T.HH[:, 0::5], st[:, 272:288])
+        S(fk, "FS", T.FS[:, 0::16], fin[:], AF.Copy)
+        mms("WB " + fk, "AUX1", [(T.AUX1[:, 0:16], T.WB[:, 15 - b:143 - b], fin[:, b::16], b == 0, b == 15) for b in range(16)])
+        for s in range(1, 5):
+            ks, key = str(s), "KEY%d" % (nstep % 2)
+            psum = T[key]
+            nstep += 1
+            nu = T.NU[:, 256 * s - 256:256 * s]
+            V(PFA + " LU", "NU" + ks, "tc", nu, T.PF[:, 0:5136].indirect(T.LU[:, 0:16]))
+            mms("IDN " + stk, key, [(psum[:, 0:256], T.IDN[:], st[:, 0:256], True, False)])
+            for c, (a0, a1) in reversed(list(enumerate(CH))):
+                if c >= VEXP:
+                    S("FS XREP", "FE%d" % c, T.FE[:, 256 * a0:256 * a1], T.FS[:, 0:4096].indirect(T.XREP[:, 16 * a0:16 * a1]), AF.Copy)
+            for c, (a0, a1) in enumerate(CH):
+                if c < VEXP:
+                    V("KEEP FS", "FE%d" % c, "scan", T.FE[:, 256 * a0:256 * a1], T.KEEP[:, 0:256 * (a1 - a0)], T.FS[:, 256 * a0:256 * a1], 0.0, AO.mult, AO.add)
+            for c, (a0, a1) in enumerate(CH):
+                V("R RZ FE%d NU%s" % (c, ks), "D%d" % c, "tt", T.D2[:, 256 * a0:256 * a1],
+                  T.R[:, 0:4112].indirect(T.NU[:, 256 * s - 256 + 16 * a0:256 * s - 256 + 16 * a1]), T.FE[:, 256 * a0:256 * a1], AO.subtract)
+                S("D%d" % c, "A%d" % c, T.A3[:, a0:a1, :], T.D2[:, 256 * a0:256 * a1], AF.Abs)
+                mms("WB A%d" % c, key, [(psum[:, 16 * a0:16 * a1], T.WB[:, 15 - b:143 - b], T.A3[:, a0:a1, 16 * b:16 * b + 16], False,
+                                         c == len(CH) - 1 and b == 15) for b in range(16)])
+            S(PFA + " LU", "NH" + ks, T.NHF[:, 256 * s - 256:256 * s], T.PF[:, 0:5136].indirect(T.LU[:, 0:16]), AF.Copy)
+            if t == 0 and s == 1:
+                late_constants()
+            if s == 1:
+                V("AUX1", "KH0", "tc", T.KH[:, 0::5], T.AUX1[:, 0:16])
+            if s > 1:
+                V("KK%d OPN%d" % (s - 1, s - 1), "HH%d" % s, "tt", T.HH[:, s - 1::5], T.KK[:, s - 2::5][:, 0:16] if False else T.KK[:, s - 2::5], opn(T, s - 1), AO.mult)
+            V("RST " + key, "SC", "scan", T.SC[:], T.RST[:], psum[:, 0:256], 0.0, AO.add, AO.min)
+            V("SC", "KH" + ks, "tc", T.KH[:, s::5], T.SC[:, 15::16])
+            V("KK4 KH" + ks, "KK" + ks, "ts", T.KK[:, s - 1::5], T.KH[:, s::5], 13, 15, AO.arith_shift_right, AO.bitwise_and)
+            V("KH" + ks, "CC", "ts", T.CC[:], T.KH[:, s::5], 8191, None, AO.bitwise_and)
+            V("XL16 KK" + ks, "FA", "tt", T.FA[:], T.KK[:, s - 1::5], T.XL16[:], AO.add)
+
+            def ne(j):
+                V("KK%s HH%d" % (ks, j), "T%d" % (j - 1) if s > 1 else "OPN1", "tt", T["T%d" % (j - 1)][:] if s > 1 else opn(T, 1),
+                  T.KK[:, s - 1::5], T.HH[:, j - 1::5], AO.not_equal)
+            ne(1)
+            V("FA", "FL", "tc", T.FL[:], T.FA[:])
+            S("FL D0 D1 D2 D3", "FS" if s < 4 else fok, T.FS[:, 0::16] if s < 4 else fo[:], T.D2[:, 0:4096].indirect(T.FL[:, 0:16]), AF.Abs)
+            for j in range(2, s + 1):
+                ne(j)
+            if s == 2:
+                V("T0 T1", "OPN2", "tt", opn(T, 2), T.T0[:], T.T1[:], AO.mult)
+            if s == 3:
+                V("T0 T1", "T0", "tt", T.T0[:], T.T0[:], T.T1[:], AO.mult)
+                V("T0 T2", "OPN3", "tt", opn(T, 3), T.T0[:], T.T2[:], AO.mult)
+            if s == 4:
+                V("T0 T1", "T0", "tt", T.T0[:], T.T0[:], T.T1[:], AO.mult)
+                V("T2 T3", "T2", "tt", T.T2[:], T.T2[:], T.T3[:], AO.mult)
+                V("T0 T2", "OPN4", "tt", opn(T, 4), T.T0[:], T.T2[:], AO.mult)
+            else:
+                V("CC OPN" + ks, "LST%d" % (s + 1), "tt", T.LST[:, 16 * s:16 * s + 16], T.CC[:], opn(T, s), AO.mult)
+                V("LST%d" % (s + 1), "LU", "tc", T.LU[:], T.LST[:, 16 * s:16 * s + 16])
+        if t < 2:
+            send((rank + 1) % nrank, fo[:], T["FIN%d" % (t + 1)][:], "aF%d" % (t + 1), fok)
+        else:
+            dma("Y", fok, "yf", T.yf[:], fo[:])
+        KHA, KKA = "KH0 KH1 KH2 KH3 KH4", "KK4 KK1 KK2 KK3 KK4"
+        OPA, HHA = "OPN OPN1 OPN2 OPN3 OPN4", "HH HH1 HH2 HH3 HH4"
+        LSA, NHA = "LST1 LST2 LST3 LST4", "NH1 NH2 NH3 NH4"
+        Q = [T.QB[:, 80 * i:80 * i + 80] for i in range(6)]
+        V(OPA, "CLB", "tt", T.CLB[:], T.OPN[:, 0:80], T.OPN[:, 1:81], AO.subtract)
+        V(KHA, "DP", "ts", T.DP[:], T.KH[:], 17, 1, AO.arith_shift_right, AO.bitwise_and)
+        V("CLB " + KKA, "QB3", "tt", Q[3], T.CLB[:], T.KK[:], AO.mult)
+        V("DP", "AS", "tt", T.AS[:, 0:79], T.DP[:, 0:79], T.DP[:, 1:80], AO.add)
+        V("KEEP5 QB3", "KSS", "scan", T.KSS[:], T.KEEP5[:, 0:80], Q[3], 0.0, AO.mult, AO.add)
+        V(HHA, "H16", "ts", T.H16[:], T.HH[:], 16.0, None, AO.add)
+        if t > 0:
+            V("AS ZA", "AS", "ts", T.AS[:], T.AS[:], T.ZA[:, 0:1], None, AO.add)
+        for j in range(4):
+            V("H16 KSS", "EQB", "tt", T.EQB[:, j::5], T.H16[:, j::5], T.KSS[:, 4::5], AO.is_equal)
+        V("AS", "OD", "ts", T.OD[:], T.AS[:], 1, None, AO.bitwise_and)
+        V("CLB SI", "QB2", "tt", Q[2], T.CLB[:], T.SI[:], AO.mult)
+        V("EQB " + OPA, "GB", "tt", T.GB[:], T.EQB[:], T.OPN[:, 0:80], AO.mult)
+        V(LSA, "Q0", "ts", T.Q0[:], T.LST[:], 0.0, None, AO.is_equal)
+        V("GB SI", "QB0", "tt", Q[0], T.GB[:], T.SI[:], AO.mult)
+        V("GB " + KKA, "QB1", "tt", Q[1], T.GB[:], T.KK[:], AO.mult)
+        V("GB OD", "QB4", "tt", Q[4], T.GB[:], T.OD[:], AO.mult)
+        V("GB OD", "QB5", "tt", Q[5], T.GB[:], T.OD[:], AO.mult)
+        V("KEEP5 QB0 QB1 QB2 QB3 QB4 QB5", "QS", "scan", T.QS[:], T.KEEP5[:], T.QB[:], 0.0, AO.mult, AO.add)
+        V("KEEP5 GB", "PG", "scan", T.PG[:], T.KEEP5[:, 0:80], T.GB[:], 0.0, AO.mult, AO.add)
+        V("QS", "DF", "tt", T.DF[:], T.QS[:, 164:320:5], T.QS[:, 4:160:5], AO.subtract)
+        V("PG " + OPA, "UB", "tt", T.UB[:], T.PG[:], T.OPN[:, 0:80], AO.mult)
+        V("DF QS", "DG", "tt", T.DG[:], T.DF[:], T.QS[:, 324:480:5], AO.mult)
+        V(KKA, "KM", "ts", T.KM[:], T.KK[:], -32.0, None, AO.add)
+        V("DG QS", "RS", "tt", T.RS[:], T.DG[:], T.QS[:, 4:160:5], AO.add)
+        V("Q0 TR", "Q1", "tt", T.Q1[:], T.Q0[:], T.TR[:], AO.mult)
+        V("RS", "LKD", "tc", T.LKD[:], T.RS[:, 16:32])
+        V("RS XL", "LJA", "tt", T.LJA[:], T.RS[:, 0:16], T.XL[:], AO.add)
+        S("OHW LKD", "OHD", T.OHD[:], T.OHW[:, 0:48].indirect(T.LKD[:, 0:16]), AF.Copy)
+        V("KM UB", "KU", "tt", T.KU[:], T.KM[:], T.UB[:], AO.mult)
+        V("LJA", "LJD", "tc", T.LJD[:], T.LJA[:])
+        V("OHD LJD " + NHA, "SEL", "tt", T.SEL[:], T.NHF[:, 0:1024].indirect(T.LJD[:, 0:16]), T.OHD[:], AO.mult)
+        mms("BO SEL", "AUX0", [(T.AUX0[:, 0:256], T.BO[:], T.SEL[:], True, True)])
+        for s in range(4):
+            V("KU", "LC", "ts", T.LC[:, 16 * s:16 * s + 16], T.KU[:, s::5], 32.0, None, AO.add)
+        V("Q1 " + LSA, "Q2", "tt", T.Q2[:], T.Q1[:], T.LST[:], AO.add)
+        if t < 2:
+            V(OPA, "ZR", "red", T.ZR[:, 0:1], T.OPN[:, 4:80:5], AxisListType.X, AO.add)
+            mms("ONE ZR", "AUX1", [(T.AUX1[:, 0:1], T.ONE[:], T.ZR[:, 0:1], True, True)])
+        V("Q2", "SL", "tc", T.SL[:], T.Q2[:])
+        for s in range(4):
+            V("AUX0 " + NHA, "DL", "tt", T.DL[:, 256 * s:256 * s + 256], T.AUX0[:, 0:256], T.NHF[:, 256 * s:256 * s + 256], AO.subtract)
+        V("OHW LC DL", "BB", "tt", T.BB[:], T.OHW[:, 0:48].indirect(T.LC[:, 0:64]), T.DL[:], AO.mult)
+        if t == 0:
+            V("AUX1", "ZA", "tc", T.ZA[:, 0:1], T.AUX1[:, 0:1])
+        elif t == 1:
+            V("AUX1 ZA", "ZA", "tt", T.ZA[:, 0:1], T.AUX1[:, 0:1], T.ZA[:, 0:1], AO.add)
+        V(NHA + " BB SL", PFA, "tt", T.PF[:, 0:5136].indirect(T.SL[:, 0:64]), T.NHF[:], T.BB[:], AO.add)
+    for q in range(4):
+        c0, c1, k = 512 * q, 512 * q + 512, str(q)
+        S("PFH" + k, "HP" + k, T["HP" + k][:], T.PF[:, 2049 + c0:2049 + c1], AF.Copy, scale=4096.0)
+        V("HP%s PFL%s" % (k, k), "YO" + k, "tt", T.YO[:, c0:c1], T["HP" + k][:], T.PF[:, 1 + c0:1 + c1], AO.add)
+        dma("Y", "YO" + k, "yp", T.yp[:, c0:c1], T.YO[:, c0:c1])
+    for sem in SEMAPHORES:
+        if cnt[sem] and sem != "ls":
+            need("G", sem, cnt[sem])
+    need("G", "ls", cnt["ls"])
+    for sem in ("aS1", "aS2", "aF1", "aF2"):
+        need("G", sem, narr)
+
+
+def opn(T, s):
+    return T.OPN[:, s:80:5]
+
+
+def unpack_lo(V, T, q):
+    c0, c1, k = 512 * q, 512 * q + 512, str(q)
+    V("PFT PK%d HP%s" % (q // 2, k), "PFL" + k, "tt", T.PF[:, 1 + c0:1 + c1], T["HP" + k][:], T.PK[:, c0:c1], AO.subtract) if False else \
+        V("PFT PK%d HP%s" % (q // 2, k), "PFL" + k, "tt", T.PF[:, 1 + c0:1 + c1], T.PK[:, c0:c1], T["HP" + k][:], AO.subtract)

@@ -3,8 +3,8 @@ import comms_topo
 
 AO = AluOpType
 AF = ActivationFunctionType
-CH = [(0, 5), (5, 10), (10, 14), (14, 16)]
-VEXP = 2
+CH = [(0, 5), (5, 8)]
+FE = {"v": (0, 3), "a": (3, 5), "b": (5, 8)}
 
 F32, BF, I32, U16 = "float32", "bfloat16", "int32", "uint16"
 SCRATCH = {}
@@ -15,24 +15,25 @@ def _s(name, cols, dtype, where="sbuf"):
 
 
 for _n, _c, _d in [
-        ("R", 4112, BF), ("PF", 5136, F32), ("PK", 2048, I32), ("TI", 2048, I32), ("YO", 2048, F32),
+        ("R", 4096, BF), ("PF", 5136, F32), ("PK", 2048, I32), ("TI", 2048, I32), ("YO", 2048, F32),
         ("JI", [16, 16], I32), ("JF", [16, 16], F32), ("JT", [16, 128], F32), ("SRI", 256, I32), ("SRB", 256, BF),
         ("SRG", 256, BF), ("FX0", 256, BF), ("FIN1", 256, BF), ("FIN2", 256, BF),
         ("FO0", 256, BF), ("FO1", 256, BF), ("FO2", 256, BF),
         ("ST0", 288, F32), ("ST1", 288, F32), ("ST2", 288, F32),
-        ("FS", 4096, BF), ("FE", 4096, BF), ("D2", 4096, BF), ("A3", [16, 256], BF),
-        ("NU", 1024, U16), ("NHF", 1024, F32), ("DL", 1024, F32), ("BB", 1024, F32), ("SEL", 256, F32), ("OHD", 256, F32),
-        ("SC", 256, F32), ("KH", 80, I32), ("KK", 80, I32), ("HH", 80, F32), ("OPN", 96, F32), ("LST", 64, F32),
-        ("CC", 16, I32), ("T0", 16, F32), ("T1", 16, F32), ("T2", 16, F32), ("T3", 16, F32), ("FA", 16, I32),
-        ("FL", 16, U16), ("LU", 16, U16), ("DP", 80, I32), ("AS", 80, I32), ("OD", 80, I32), ("CLB", 80, F32),
-        ("CK", 80, F32), ("KSS", 80, F32), ("H16", 80, F32), ("EQB", 80, F32), ("GB", 80, F32), ("PG", 80, F32), ("UB", 80, F32),
+        ("FS", 4096, BF), ("WW", 8192, BF), ("A3", [16, 256], BF),
+        ("NU", 1024, U16), ("NHF", 1024, F32), ("NP", 1024, F32), ("OHM", 1024, F32), ("BB", 1024, F32), ("SEL", 256, F32), ("OHD", 256, F32),
+        ("SC", 256, F32), ("KH", 80, I32), ("HK", 96, I32), ("OPN", 96, F32), ("LST", 64, F32),
+        ("CCH", 48, I32), ("OX", 16, F32), ("OXT", 16, F32), ("XLW", 16, F32),
+        ("T0", 16, F32), ("T1", 16, F32), ("T2", 16, F32), ("T3", 16, F32), ("FA", 16, I32),
+        ("FL", 16, U16), ("LUH", 64, U16), ("DP", 80, I32), ("AS", 80, I32), ("OD", 80, I32), ("CLB", 80, F32),
+        ("KSS", 80, F32), ("H16", 96, F32), ("EQB", 80, F32), ("GB", 80, F32), ("PG", 80, F32), ("UB", 80, F32),
         ("QB", 480, F32), ("QS", 480, F32), ("DF", 32, F32), ("DG", 32, F32), ("RS", 32, F32), ("LJA", 16, F32), ("LJD", 16, U16), ("LKD", 16, U16),
-        ("KM", 80, F32), ("KU", 80, F32), ("LC", 64, U16), ("Q0", 64, F32), ("Q1", 64, F32), ("Q2", 64, F32), ("SL", 64, U16),
-        ("ZR", 1, F32), ("ZA", 1, F32), ("ZB", 1, F32),
+        ("KU", 80, F32), ("LC", 64, U16), ("Q0", 64, F32), ("Q1", 64, F32), ("Q2", 64, F32), ("SL", 64, U16),
+        ("ZR", 1, F32), ("ZA", 1, F32),
         ("IM", 160, F32), ("IG", 128, F32), ("IPI", 2, I32), ("IQI", 2, I32), ("IGI", 2, I32), ("CF", 4, F32),
         ("IDN", 128, F32), ("WB", 144, BF), ("BO", 128, F32), ("ONE", 128, F32), ("L8", 128, BF), ("MG", 8, F32), ("E16", 16, F32),
-        ("OHW", 48, F32), ("KEEP", 1280, BF), ("RST", 256, F32), ("KEEP5", 480, F32), ("XRI", 256, I32), ("XREP", 256, U16),
-        ("IA", 16, F32), ("XL", 16, F32), ("XL16", 16, F32), ("TRI", 64, F32), ("TR", 64, F32), ("SI", 80, F32), ("PLC", 256, F32),
+        ("OHW", 32, F32), ("OHC", 32, F32), ("KEEP", 768, BF), ("RST", 128, F32), ("KEEP5", 480, F32), ("XRI", 128, I32), ("XREP", 128, U16),
+        ("IA", 16, F32), ("XL", 16, F32), ("TRI", 64, F32), ("TR", 64, F32), ("SI", 80, F32), ("PLC", 256, F32),
         ("QK", 256, F32), ("XZ", 256, F32), ("XA", 256, F32), ("XB", 256, F32), ("XC", 256, F32)]:
     _s(_n, _c, _d)
 for _n in ["KEY0", "KEY1", "AUX0", "AUX1", "HP0", "HP1", "HP2", "HP3"]:
@@ -119,24 +120,35 @@ def rank_program(g, core, T, topo):
 
     dma("Y", "", "JI", T.JI[:, :, :], T.jc[:])
     dma("S", "", "SRI", T.SRI[0:8, :], T.sr[:])
-    dma("S", "", "FX0", T.FX0[:], T.fx[:])
     dma("Y", "", "PK0", T.PK[:, 0:1024], T.pk[:, 0:1024])
+    dma("S", "", "FX0", T.FX0[:], T.fx[:])
     dma("Y", "", "PK1", T.PK[:, 1024:2048], T.pk[:, 1024:2048])
-    dma("Y", "", "R", T.R[:, 0:4096], T.rt[:])
+    dma("Y", "", "R", T.R[:], T.rt[:])
 
-    big = {"allow_small_or_imprecise_dtypes": True}
-
-    def iota(name, pat, base, cm, out=None):
-        run("G", "", name, "iota", T[name][:] if out is None else out, pat, base, cm, **({} if name in ("IPI", "XRI") else big))
+    def iota(name, pat, base, cm, key=None):
+        run("G", "", key or name, "iota", T[name][:], pat, base, cm,
+            **({} if SCRATCH[name][2] == I32 else {"allow_small_or_imprecise_dtypes": True}))
     iota("IPI", [[0, 2]], 0, 1)
     iota("IM", [[1, 160]], 0, 0)
     iota("IG", [[1, 8], [0, 16]], 0, 0)
-    iota("PLC", [[0, 16], [8192, 16]], -16777215, 0)
+    iota("XZ", [[0, 256]], 0, 0)
+    iota("KEEP", [[0, 768]], 1, 0)
     iota("QK", [[0, 16], [1, 16]], 0, 0)
+    iota("PLC", [[0, 16], [8192, 16]], -16777215, 0)
+    iota("XRI", [[16, 128]], 0, 0)
     iota("IA", [[16, 16]], 0, 0)
-    iota("XRI", [[16, 256]], 0, 0)
+    iota("RST", [[0, 128]], 0, 0)
+    iota("FS", [[0, 4096]], 0, 0, "FS0 FS1")
+    iota("OPN", [[0, 96]], 1, 0)
+    iota("HK", [[0, 96]], 0, 0)
     iota("TRI", [[256, 4], [16, 16]], 4097, 0)
     iota("SI", [[0, 16], [256, 5]], 0, 0)
+    iota("KEEP5", [[0, 480]], 1, 0)
+    iota("ONE", [[0, 128]], 1, 0)
+    iota("AS", [[0, 80]], 0, 0)
+    iota("EQB", [[0, 80]], 0, 0)
+    iota("OHW", [[0, 32]], 0, 0)
+    iota("OHC", [[0, 32]], 1, 0)
     V("IPI", "IQI", "ts", T.IQI[:], T.IPI[:], 15, None, AO.bitwise_and)
     V("IPI", "IGI", "ts", T.IGI[:], T.IPI[:], 4, None, AO.arith_shift_right)
     V("IPI", "CF0", "tc", T.CF[:, 0:1], T.IPI[:, 0:1])
@@ -144,28 +156,54 @@ def rank_program(g, core, T, topo):
     V("IGI", "CF2", "tc", T.CF[:, 2:3], T.IGI[:, 0:1])
     V("IGI", "CF3", "ts", T.CF[:, 3:4], T.IGI[:, 0:1], 16.0, 15.0, AO.mult, AO.add)
     p_c, q_c, g_c, e_c = [T.CF[:, i:i + 1] for i in range(4)]
-    V("IG CF0", "L8", "ts", T.L8[0:8, :], T.IG[0:8, :], T.CF[0:8, 0:1], None, AO.is_equal)
-    V("IM CF3", "WB", "ts", T.WB[:, 0:143], T.IM[:, 0:143], e_c, 131072.0, AO.is_equal, AO.mult)
     V("IM CF2", "MG", "ts", T.MG[:], T.IM[:, 0:8], g_c, None, AO.is_equal)
+    V("IM CF3", "WB", "ts", T.WB[:, 0:143], T.IM[:, 0:143], e_c, 131072.0, AO.is_equal, AO.mult)
     V("IM CF1", "E16", "ts", T.E16[:], T.IM[:, 0:16], q_c, None, AO.is_equal)
-    V("", "KEEP", "memset", T.KEEP[:], 1.0)
-    V("", "XZ", "memset", T.XZ[:], 0.0)
-    V("", "KEEP", "memset", T.KEEP[:, 0::16], 0.0)
+    V("IG CF0", "L8", "ts", T.L8[0:8, :], T.IG[0:8, :], T.CF[0:8, 0:1], None, AO.is_equal)
+    V("IM CF0", "IDN", "ts", T.IDN[:], T.IM[:, 0:128], p_c, None, AO.is_equal)
 
+    def late_constants():
+        V("IG CF2", "BO", "ts", T.BO[:], T.IG[:], g_c, None, AO.is_equal)
+        V("IM CF1", "OHW", "ts", T.OHW[:, 16:32], T.IM[:, 0:16], q_c, None, AO.is_equal)
+        V("IM CF1", "OHC", "ts", T.OHC[:, 16:32], T.IM[:, 0:16], q_c, None, AO.not_equal)
+        V("TRI CF1", "TR", "ts", T.TR[:], T.TRI[:], q_c, None, AO.add)
+        V("", "KEEP5", "memset", T.KEEP5[:, 0::5], 0.0)
+
+    def unpack_hi(q):
+        c0, c1, k = 512 * q, 512 * q + 512, str(q)
+        V("PK%d" % (q // 2), "TI" + k, "ts", T.TI[:, c0:c1], T.PK[:, c0:c1], 12, None, AO.arith_shift_right)
+        V("PFT TI" + k, "PFH" + k, "tc", T.PF[:, 2049 + c0:2049 + c1], T.TI[:, c0:c1])
+        S("PFH" + k, "HP" + k, T["HP" + k][:], T.PF[:, 2049 + c0:2049 + c1], AF.Copy, scale=4096.0)
+
+    def unpack_lo(q):
+        c0, c1, k = 512 * q, 512 * q + 512, str(q)
+        V("PFT PK%d HP%s" % (q // 2, k), "PFL" + k, "tt", T.PF[:, 1 + c0:1 + c1], T.PK[:, c0:c1], T["HP" + k][:], AO.subtract)
+    PFA = "PFT " + " ".join("PFH%d PFL%d" % (q, q) for q in range(4))
+
+    V("JI", "JF", "tc", T.JF[:, :, :], T.JI[:, :, :])
+    for h in range(8):
+        S("JF MG", "JT%d" % h, T.JT[:, :, 16 * h:16 * h + 16], T.JF[:, :, :], AF.Identity, scale=T.MG[:, h:h + 1])
     V("SRI", "SRB", "tc", T.SRB[0:8, :], T.SRI[0:8, :])
     mms("L8 SRB", "AUX0", [(T.AUX0[:, 0:256], T.L8[0:8, :], T.SRB[0:8, :], True, True)])
-    V("JI", "JF", "tc", T.JF[:, :, :], T.JI[:, :, :])
+    V("", "PFT", "memset", T.PF[:, 0:16], 4096.0)
+    V("", "PFT", "memset", T.PF[:, 4096:4112], 0.0)
+    V("XRI", "XREP", "tc", T.XREP[:], T.XRI[:])
     V("AUX0", "SRG", "tc", T.SRG[:], T.AUX0[:, 0:256])
     mms("WB SRG", "AUX1", [(T.AUX1[:, 0:16], T.WB[:, 15 - b:143 - b], T.SRG[:, b::16], b == 0, b == 15) for b in range(16)])
-    for h in range(8):
-        V("JF MG", "JT", "ts", T.JT[:, :, 16 * h:16 * h + 16], T.JF[:, :, :], T.MG[:, h:h + 1], None, AO.mult)
-    mms("JT E16", "KEY1", [(T.KEY1[:, 16 * a:16 * a + 16], T.JT[:, a, :], T.E16[:], True, True) for a in range(16)])
-    V("AUX1", "XZ", "ts", T.XZ[:, 0::16], T.AUX1[:, 0:16], 2.0 ** -21, None, AO.mult)
+    mms("JT0 JT1 JT2 JT3 JT4 JT5 JT6 JT7 E16", "KEY1", [(T.KEY1[:, 16 * a:16 * a + 16], T.JT[:, a, :], T.E16[:], True, True) for a in range(16)])
+    V("KEEP", "KEEP", "memset", T.KEEP[:, 0::16], 0.0)
+    V("RST", "RST", "memset", T.RST[:, 0::16], 67108864.0)
+    V("IA CF1", "XL", "ts", T.XL[:], T.IA[:], q_c, None, AO.add)
+    V("XL", "XLW", "ts", T.XLW[:, 0:8], T.XL[:, 0:8], 16.0, None, AO.mult)
+    V("XL", "XLW", "ts", T.XLW[:, 8:16], T.XL[:, 0:8], 16.0, None, AO.mult)
+    V("AUX1 XZ", "XZ", "ts", T.XZ[:, 0::16], T.AUX1[:, 0:16], 2.0 ** -21, None, AO.mult)
     V("AUX1", "ST0", "ts", T.ST0[:, 272:288], T.AUX1[:, 0:16], 2.0 ** -21, None, AO.mult)
     V("KEEP XZ", "XA", "scan", T.XA[:], T.KEEP[:, 0:256], T.XZ[:], 0.0, AO.mult, AO.add)
     V("XA QK", "XB", "tt", T.XB[:], T.XA[:], T.QK[:], AO.is_equal)
-    V("KEY1 PLC", "ST0", "tt", T.ST0[:, 0:256], T.KEY1[:, 0:256], T.PLC[:], AO.add)
+    unpack_hi(0)
+    unpack_hi(1)
     V("KEY1 XB", "XC", "tt", T.XC[:], T.KEY1[:, 0:256], T.XB[:], AO.mult)
+    V("KEY1 PLC", "ST0", "tt", T.ST0[:, 0:256], T.KEY1[:, 0:256], T.PLC[:], AO.add)
     V("KEEP XC", "XA", "scan", T.XA[:], T.KEEP[:, 0:256], T.XC[:], 0.0, AO.mult, AO.add)
     V("XA", "ST0", "ts", T.ST0[:, 256:272], T.XA[:, 15::16], 1.0, None, AO.add)
     send((rank + 1) % nrank, T.ST0[:], T.ST1[:], "aS1", "ST0")
@@ -173,162 +211,227 @@ def rank_program(g, core, T, topo):
     Wr["ST1"], Wr["ST2"] = {"aS1": narr}, {"aS2": narr}
     Wr["FIN1"], Wr["FIN2"] = {"aF1": narr}, {"aF2": narr}
 
-    V("", "FS", "memset", T.FS[:], 0.0)
-    V("IM CF0", "IDN", "ts", T.IDN[:], T.IM[:, 0:128], p_c, None, AO.is_equal)
-    V("", "RST", "memset", T.RST[:], 0.0)
-    V("", "PFT", "memset", T.PF[:, 0:16], 4096.0)
-    V("XRI", "XREP", "tc", T.XREP[:], T.XRI[:])
-    V("", "RST", "memset", T.RST[:, 0::16], 67108864.0)
-    V("", "PFT", "memset", T.PF[:, 4080:5136], 4096.0)
-    V("", "RZ", "memset", T.R[:, 4096:4112], 0.0)
-    V("IA CF1", "XL", "ts", T.XL[:], T.IA[:], q_c, None, AO.add)
-    V("", "OPN", "memset", T.OPN[:], 1.0)
-    V("XL", "XL16", "ts", T.XL16[:], T.XL[:], 16.0, None, AO.mult)
-    V("", "KK4", "memset", T.KK[:], -16)
+    def a5(buf, X, s):
+        return buf[:, 40 * X + s:40 * X + 40:5]
 
-    for q in range(4):
-        c0, c1, k = 512 * q, 512 * q + 512, str(q)
-        V("PK%d" % (q // 2), "TI" + k, "ts", T.TI[:, c0:c1], T.PK[:, c0:c1], 12, None, AO.arith_shift_right)
-        if q > 0:
-            unpack_lo(V, T, q - 1)
-        V("PFT TI" + k, "PFH" + k, "tc", T.PF[:, 2049 + c0:2049 + c1], T.TI[:, c0:c1])
-        S("PFH" + k, "HP" + k, T["HP" + k][:], T.PF[:, 2049 + c0:2049 + c1], AF.Copy, scale=4096.0)
-    unpack_lo(V, T, 3)
-    PFA = "PFT " + " ".join("PFH%d PFL%d" % (q, q) for q in range(4))
+    def opn(s):
+        return T.OPN[:, s:80:5]
 
-    def late_constants():
-        V("IG CF2", "BO", "ts", T.BO[:], T.IG[:], g_c, None, AO.is_equal)
-        V("", "ONE", "memset", T.ONE[:], 1.0)
-        V("IM CF1", "OHW", "ts", T.OHW[:, 0:16], T.IM[:, 0:16], q_c, None, AO.is_equal)
-        V("IM CF1", "OHW", "ts", T.OHW[:, 16:32], T.IM[:, 0:16], q_c, None, AO.is_equal)
-        V("", "OHW", "memset", T.OHW[:, 32:48], 0.0)
-        V("", "KEEP5", "memset", T.KEEP5[:], 1.0)
-        V("TRI CF1", "TR", "ts", T.TR[:], T.TRI[:], q_c, None, AO.add)
-        V("", "SI", "memset", T.SI[:, 4::5], 0.0)
-        V("", "KEEP5", "memset", T.KEEP5[:, 0::5], 0.0)
-        V("", "AS", "memset", T.AS[:], 0)
-        V("", "EQB", "memset", T.EQB[:], 0.0)
-        V("", "HH", "memset", T.HH[:, 4::5], 0.0)
+    def win(X):
+        return T.WW[:, 4096 * X:4096 * X + 4096]
 
-    nstep = 0
+    def lists_of_visit(t):
+        V("ST%d" % t, "LU01 LU11", "tc", T.LUH[:, 0:16], T["ST%d" % t][:, 256:272])
+
+    unpack_lo(0)
+    unpack_hi(2)
+    unpack_lo(1)
+    unpack_hi(3)
+    unpack_lo(2)
+    lists_of_visit(0)
+    unpack_lo(3)
     for t in range(3):
-        st = T["ST%d" % t]
-        stk = "ST%d" % t
+        st, stk = T["ST%d" % t], "ST%d" % t
         fin, fk = (T.FX0, "FX0") if t == 0 else (T["FIN%d" % t], "FIN%d" % t)
         fo, fok = T["FO%d" % t], "FO%d" % t
-        V(stk, "LST1", "tc", T.LST[:, 0:16], st[:, 256:272])
-        V(stk, "LU", "tc", T.LU[:], st[:, 256:272])
-        V(stk, "HH1", "tc", T.HH[:, 0::5], st[:, 272:288])
-        S(fk, "FS", T.FS[:, 0::16], fin[:], AF.Copy)
-        mms("WB " + fk, "AUX1", [(T.AUX1[:, 0:16], T.WB[:, 15 - b:143 - b], fin[:, b::16], b == 0, b == 15) for b in range(16)])
-        for s in range(1, 5):
-            ks, key = str(s), "KEY%d" % (nstep % 2)
-            psum = T[key]
-            nstep += 1
-            nu = T.NU[:, 256 * s - 256:256 * s]
-            V(PFA + " LU", "NU" + ks, "tc", nu, T.PF[:, 0:5136].indirect(T.LU[:, 0:16]))
-            mms("IDN " + stk, key, [(psum[:, 0:256], T.IDN[:], st[:, 0:256], True, False)])
-            for c, (a0, a1) in reversed(list(enumerate(CH))):
-                if c >= VEXP:
-                    S("FS XREP", "FE%d" % c, T.FE[:, 256 * a0:256 * a1], T.FS[:, 0:4096].indirect(T.XREP[:, 16 * a0:16 * a1]), AF.Copy)
-            for c, (a0, a1) in enumerate(CH):
-                if c < VEXP:
-                    V("KEEP FS", "FE%d" % c, "scan", T.FE[:, 256 * a0:256 * a1], T.KEEP[:, 0:256 * (a1 - a0)], T.FS[:, 256 * a0:256 * a1], 0.0, AO.mult, AO.add)
-            for c, (a0, a1) in enumerate(CH):
-                V("R RZ FE%d NU%s" % (c, ks), "D%d" % c, "tt", T.D2[:, 256 * a0:256 * a1],
-                  T.R[:, 0:4112].indirect(T.NU[:, 256 * s - 256 + 16 * a0:256 * s - 256 + 16 * a1]), T.FE[:, 256 * a0:256 * a1], AO.subtract)
-                S("D%d" % c, "A%d" % c, T.A3[:, a0:a1, :], T.D2[:, 256 * a0:256 * a1], AF.Abs)
-                mms("WB A%d" % c, key, [(psum[:, 16 * a0:16 * a1], T.WB[:, 15 - b:143 - b], T.A3[:, a0:a1, 16 * b:16 * b + 16], False,
-                                         c == len(CH) - 1 and b == 15) for b in range(16)])
-            S(PFA + " LU", "NH" + ks, T.NHF[:, 256 * s - 256:256 * s], T.PF[:, 0:5136].indirect(T.LU[:, 0:16]), AF.Copy)
-            if t == 0 and s == 1:
-                late_constants()
-            if s == 1:
-                V("AUX1", "KH0", "tc", T.KH[:, 0::5], T.AUX1[:, 0:16])
-            if s > 1:
-                V("KK%d OPN%d" % (s - 1, s - 1), "HH%d" % s, "tt", T.HH[:, s - 1::5], T.KK[:, s - 2::5][:, 0:16] if False else T.KK[:, s - 2::5], opn(T, s - 1), AO.mult)
-            V("RST " + key, "SC", "scan", T.SC[:], T.RST[:], psum[:, 0:256], 0.0, AO.add, AO.min)
-            V("SC", "KH" + ks, "tc", T.KH[:, s::5], T.SC[:, 15::16])
-            V("KK4 KH" + ks, "KK" + ks, "ts", T.KK[:, s - 1::5], T.KH[:, s::5], 13, 15, AO.arith_shift_right, AO.bitwise_and)
-            V("KH" + ks, "CC", "ts", T.CC[:], T.KH[:, s::5], 8191, None, AO.bitwise_and)
-            V("XL16 KK" + ks, "FA", "tt", T.FA[:], T.KK[:, s - 1::5], T.XL16[:], AO.add)
 
-            def ne(j):
-                V("KK%s HH%d" % (ks, j), "T%d" % (j - 1) if s > 1 else "OPN1", "tt", T["T%d" % (j - 1)][:] if s > 1 else opn(T, 1),
-                  T.KK[:, s - 1::5], T.HH[:, j - 1::5], AO.not_equal)
-            ne(1)
-            V("FA", "FL", "tc", T.FL[:], T.FA[:])
-            S("FL D0 D1 D2 D3", "FS" if s < 4 else fok, T.FS[:, 0::16] if s < 4 else fo[:], T.D2[:, 0:4096].indirect(T.FL[:, 0:16]), AF.Abs)
-            for j in range(2, s + 1):
-                ne(j)
-            if s == 2:
-                V("T0 T1", "OPN2", "tt", opn(T, 2), T.T0[:], T.T1[:], AO.mult)
-            if s == 3:
-                V("T0 T1", "T0", "tt", T.T0[:], T.T0[:], T.T1[:], AO.mult)
-                V("T0 T2", "OPN3", "tt", opn(T, 3), T.T0[:], T.T2[:], AO.mult)
-            if s == 4:
-                V("T0 T1", "T0", "tt", T.T0[:], T.T0[:], T.T1[:], AO.mult)
-                V("T2 T3", "T2", "tt", T.T2[:], T.T2[:], T.T3[:], AO.mult)
-                V("T0 T2", "OPN4", "tt", opn(T, 4), T.T0[:], T.T2[:], AO.mult)
+        def pf(X, s):
+            c0 = 256 * s - 256 + 128 * X
+            V("%s LU%d%d" % (PFA, X, s), "NU%d%d" % (X, s), "tc", T.NU[:, c0:c0 + 128], T.PF[:, 0:4112].indirect(T.LUH[:, 16 * s - 16 + 8 * X:16 * s - 8 + 8 * X]))
+
+        def pay(X):
+            mms("IDN " + stk, "KEY%d" % X, [(T["KEY%d" % X][:, 0:128], T.IDN[:], st[:, 128 * X:128 * X + 128], True, False)])
+
+        def fe(X, i):
+            c0, c1 = 256 * FE[i][0], 256 * FE[i][1]
+            if i == "v":
+                V("KEEP FS%d" % X, "WF%dv" % X, "scan", T.WW[:, 4096 * X + c0:4096 * X + c1], T.KEEP[:, 0:c1 - c0],
+                  T.FS[:, 2048 * X + c0:2048 * X + c1], 0.0, AO.mult, AO.add)
             else:
-                V("CC OPN" + ks, "LST%d" % (s + 1), "tt", T.LST[:, 16 * s:16 * s + 16], T.CC[:], opn(T, s), AO.mult)
-                V("LST%d" % (s + 1), "LU", "tc", T.LU[:], T.LST[:, 16 * s:16 * s + 16])
+                S("XREP FS%d" % X, "WF%d%s" % (X, i), T.WW[:, 4096 * X + c0:4096 * X + c1],
+                  T.FS[:, 2048 * X:2048 * X + 2048].indirect(T.XREP[:, c0 // 16:c1 // 16]), AF.Copy)
+
+        def gather(X, i, s):
+            c0, c1, n0 = 256 * CH[i][0], 256 * CH[i][1], 256 * s - 256 + 128 * X
+            V("R %s NU%d%d" % ("WF%dv WF%da" % (X, X) if i == 0 else "WF%db" % X, X, s), "WD%d%d" % (X, i), "tt",
+              T.WW[:, 4096 * X + 2048 + c0:4096 * X + 2048 + c1],
+              T.R[:, 0:4096].indirect(T.NU[:, n0 + c0 // 16:n0 + c1 // 16]), T.WW[:, 4096 * X + c0:4096 * X + c1], AO.subtract)
+
+        def dist(X, i):
+            a0, a1 = CH[i]
+            S("WD%d%d" % (X, i), "A%d%d" % (X, i), T.A3[:, 8 * X + a0:8 * X + a1, :], T.WW[:, 4096 * X + 2048 + 256 * a0:4096 * X + 2048 + 256 * a1], AF.Abs)
+            mms("WB A%d%d" % (X, i), "KEY%d" % X, [(T["KEY%d" % X][:, 16 * a0:16 * a1], T.WB[:, 15 - b:143 - b],
+                T.A3[:, 8 * X + a0:8 * X + a1, 16 * b:16 * b + 16], False, i == len(CH) - 1 and b == 15) for b in range(16)])
+
+        def nh(s):
+            S("%s LU0%d LU1%d" % (PFA, s, s), "NH%d" % s, T.NHF[:, 256 * s - 256:256 * s], T.PF[:, 0:4112].indirect(T.LUH[:, 16 * s - 16:16 * s]), AF.Copy)
+
+        def choose(X, s, fill=()):
+            k = "%d%d" % (X, s)
+            c16 = slice(16 * s - 16 + 8 * X, 16 * s - 8 + 8 * X)
+            fill = list(fill)
+            h = (len(fill) + 1) // 2
+            V("RST KEY%d" % X, "SC%d" % X, "scan", T.SC[:, 128 * X:128 * X + 128], T.RST[:], T["KEY%d" % X][:, 0:128], 0.0, AO.add, AO.min)
+            for f in fill[:h]:
+                f()
+            V("SC%d" % X, "KH" + k, "tc", a5(T.KH, X, s), T.SC[:, 128 * X + 15:128 * X + 128:16])
+            for f in fill[h:]:
+                f()
+            V("KH" + k, "HK" + k, "ts", a5(T.HK, X, s), a5(T.KH, X, s), 13, 15, AO.arith_shift_right, AO.bitwise_and)
+            if s < 4:
+                V("KH" + k, "CC" + k, "ts", T.CCH[:, c16], a5(T.KH, X, s), 8191, None, AO.bitwise_and)
+            V("OX HK" + k, "FA%d" % X, "tt", T.FA[:, 8 * X:8 * X + 8], a5(T.HK, X, s), T.OX[:, 8 * X:8 * X + 8], AO.add)
+            if s < 4:
+                V("CC" + k, "LU%d%d" % (X, s + 1), "tc", T.LUH[:, 16 * s + 8 * X:16 * s + 8 * X + 8], T.CCH[:, c16])
+            V("FA%d" % X, "FL%d" % X, "tc", T.FL[:, 8 * X:8 * X + 8], T.FA[:, 8 * X:8 * X + 8])
+            rd = "FL%d WF%dv WF%da WF%db WD%d0 WD%d1" % (X, X, X, X, X, X)
+            if s < 4:
+                S(rd, "FS%d" % X, T.FS[:, 2048 * X:2048 * X + 2048:16], win(X).indirect(T.FL[:, 8 * X:8 * X + 8]), AF.Abs)
+                pf(X, s + 1)
+                pay(X)
+            else:
+                S(rd, fok, fo[:, 128 * X:128 * X + 128], win(X).indirect(T.FL[:, 8 * X:8 * X + 8]), AF.Abs)
+
+        def keep(s):
+            H = [T.HK[:, j:80:5] for j in range(5)]
+            hk = ["HK0%d HK1%d" % (j, j) for j in range(5)]
+            todo = []
+
+            def later(*a):
+                todo.append(lambda: V(*a))
+
+            def ne(j, out, key):
+                later(hk[s] + " " + hk[j], key, "tt", out, H[s], H[j], AO.not_equal)
+
+            def mul(out, x, y, ko, kx, ky):
+                later(kx + " " + ky, ko, "tt", out, x, y, AO.mult)
+            t0, t1, t2, t3 = T.T0[:], T.T1[:], T.T2[:], T.T3[:]
+            if s == 1:
+                ne(0, opn(1), "OPN1")
+            else:
+                for j in range(s):
+                    ne(j, T["T%d" % j][:], "T%d" % j)
+                if s == 2:
+                    mul(t0, t0, opn(1), "T0", "T0", "OPN1")
+                    mul(opn(2), t0, t1, "OPN2", "T0", "T1")
+                elif s == 3:
+                    mul(t0, t0, t1, "T0", "T0", "T1")
+                    mul(t2, t2, opn(2), "T2", "T2", "OPN2")
+                    mul(opn(3), t0, t2, "OPN3", "T0", "T2")
+                else:
+                    mul(t0, t0, t1, "T0", "T0", "T1")
+                    mul(t2, t2, t3, "T2", "T2", "T3")
+                    mul(t0, t0, opn(3), "T0", "T0", "OPN3")
+                    mul(opn(4), t0, t2, "OPN4", "T0", "T2")
+            if s < 4:
+                later("OPN%d" % s, "OXT", "ts", T.OXT[:], opn(s), 2048.0, None, AO.mult)
+                later("CC0%d CC1%d OPN%d" % (s, s, s), "LST%d" % (s + 1), "tt", T.LST[:, 16 * s:16 * s + 16], T.CCH[:, 16 * s - 16:16 * s], opn(s), AO.mult)
+                later("OXT XLW", "OX", "tt", T.OX[:], T.OXT[:], T.XLW[:], AO.add)
+            return todo
+
+        pay(0)
+        pay(1)
+        for X in range(2):
+            S(fk, "FS%d" % X, T.FS[:, 2048 * X:2048 * X + 2048:16], fin[:, 128 * X:128 * X + 128], AF.Copy)
+        mms("WB " + fk, "AUX1", [(T.AUX1[:, 0:16], T.WB[:, 15 - b:143 - b], fin[:, b::16], b == 0, b == 15) for b in range(16)])
+        fe(0, "a")
+        fe(0, "b")
+        fe(1, "a")
+        pf(0, 1)
+        for s in range(1, 5):
+            for X in range(2):
+                fe(X, "v")
+                gather(X, 0, s)
+                dist(X, 0)
+                if X == 1:
+                    choose(0, s, keep(s - 1) if s > 1 else ())
+                    if s < 4:
+                        fe(0, "a")
+                elif s > 1:
+                    choose(1, s - 1)
+                    fe(1, "a")
+                gather(X, 1, s)
+                dist(X, 1)
+                if X == 0 or s < 4:
+                    fe(1 - X, "b")
+                if X == 0 and s == 1:
+                    pf(1, 1)
+                    V(stk, "LST1", "tc", T.LST[:, 0:16], st[:, 256:272])
+                    V("HK " + stk, "HK00 HK10", "tc", T.HK[:, 0:80:5], st[:, 272:288])
+                    V("XLW", "OX", "ts", T.OX[:], T.XLW[:], 2048.0, None, AO.add)
+                    V("AUX1", "KH0", "tc", T.KH[:, 0:80:5], T.AUX1[:, 0:16])
+                if X == 1:
+                    nh(s)
+        if t == 0:
+            late_constants()
+        if t < 2:
+            lists_of_visit(t + 1)
+        LSA = "LST1 LST2 LST3 LST4"
+        V(LSA, "Q0", "ts", T.Q0[:], T.LST[:], 0.0, None, AO.is_equal)
+        V("Q0 TR", "Q1", "tt", T.Q1[:], T.Q0[:], T.TR[:], AO.mult)
+        V("Q1 " + LSA, "Q2", "tt", T.Q2[:], T.Q1[:], T.LST[:], AO.add)
+        V("Q2", "SL", "tc", T.SL[:], T.Q2[:])
+        choose(1, 4)
         if t < 2:
             send((rank + 1) % nrank, fo[:], T["FIN%d" % (t + 1)][:], "aF%d" % (t + 1), fok)
         else:
             dma("Y", fok, "yf", T.yf[:], fo[:])
-        KHA, KKA = "KH0 KH1 KH2 KH3 KH4", "KK4 KK1 KK2 KK3 KK4"
-        OPA, HHA = "OPN OPN1 OPN2 OPN3 OPN4", "HH HH1 HH2 HH3 HH4"
-        LSA, NHA = "LST1 LST2 LST3 LST4", "NH1 NH2 NH3 NH4"
+        KHA = "KH0 " + " ".join("KH%d%d" % (X, s) for X in range(2) for s in range(1, 5))
+        HKA = "HK " + " ".join("HK%d%d" % (X, s) for X in range(2) for s in range(5))
+        OPA, NHA = "OPN OPN1 OPN2 OPN3 OPN4", "NH1 NH2 NH3 NH4"
         Q = [T.QB[:, 80 * i:80 * i + 80] for i in range(6)]
-        V(OPA, "CLB", "tt", T.CLB[:], T.OPN[:, 0:80], T.OPN[:, 1:81], AO.subtract)
+        k4 = keep(4)
+        for f in k4[:6]:
+            f()
+        V(HKA, "H16", "ts", T.H16[:, 0:81], T.HK[:, 0:81], 16.0, None, AO.add)
+        k4[6]()
         V(KHA, "DP", "ts", T.DP[:], T.KH[:], 17, 1, AO.arith_shift_right, AO.bitwise_and)
-        V("CLB " + KKA, "QB3", "tt", Q[3], T.CLB[:], T.KK[:], AO.mult)
-        V("DP", "AS", "tt", T.AS[:, 0:79], T.DP[:, 0:79], T.DP[:, 1:80], AO.add)
-        V("KEEP5 QB3", "KSS", "scan", T.KSS[:], T.KEEP5[:, 0:80], Q[3], 0.0, AO.mult, AO.add)
-        V(HHA, "H16", "ts", T.H16[:], T.HH[:], 16.0, None, AO.add)
+        k4[7]()
+        V("DP AS", "AS", "tt", T.AS[:, 0:79], T.DP[:, 0:79], T.DP[:, 1:80], AO.add)
+        V(OPA, "CLB", "tt", T.CLB[:], T.OPN[:, 0:80], T.OPN[:, 1:81], AO.subtract)
         if t > 0:
             V("AS ZA", "AS", "ts", T.AS[:], T.AS[:], T.ZA[:, 0:1], None, AO.add)
-        for j in range(4):
-            V("H16 KSS", "EQB", "tt", T.EQB[:, j::5], T.H16[:, j::5], T.KSS[:, 4::5], AO.is_equal)
-        V("AS", "OD", "ts", T.OD[:], T.AS[:], 1, None, AO.bitwise_and)
+        V("CLB H16", "QB3", "tt", Q[3], T.CLB[:], T.H16[:, 1:81], AO.mult)
         V("CLB SI", "QB2", "tt", Q[2], T.CLB[:], T.SI[:], AO.mult)
-        V("EQB " + OPA, "GB", "tt", T.GB[:], T.EQB[:], T.OPN[:, 0:80], AO.mult)
-        V(LSA, "Q0", "ts", T.Q0[:], T.LST[:], 0.0, None, AO.is_equal)
+        V("KEEP5 QB3", "KSS", "scan", T.KSS[:], T.KEEP5[:, 0:80], Q[3], 0.0, AO.mult, AO.add)
+        V("AS", "OD", "ts", T.OD[:], T.AS[:], 1, None, AO.bitwise_and)
+        for j in range(4):
+            V("H16 KSS EQB", "EQ%d" % j, "tt", T.EQB[:, j::5], T.H16[:, j:80:5], T.KSS[:, 3::5], AO.is_equal)
+        V("EQB EQ0 EQ1 EQ2 EQ3 " + OPA, "GB", "tt", T.GB[:], T.EQB[:], T.OPN[:, 0:80], AO.mult)
         V("GB SI", "QB0", "tt", Q[0], T.GB[:], T.SI[:], AO.mult)
-        V("GB " + KKA, "QB1", "tt", Q[1], T.GB[:], T.KK[:], AO.mult)
+        V("GB H16", "QB1", "tt", Q[1], T.GB[:], T.H16[:, 1:81], AO.mult)
         V("GB OD", "QB4", "tt", Q[4], T.GB[:], T.OD[:], AO.mult)
         V("GB OD", "QB5", "tt", Q[5], T.GB[:], T.OD[:], AO.mult)
-        V("KEEP5 QB0 QB1 QB2 QB3 QB4 QB5", "QS", "scan", T.QS[:], T.KEEP5[:], T.QB[:], 0.0, AO.mult, AO.add)
         V("KEEP5 GB", "PG", "scan", T.PG[:], T.KEEP5[:, 0:80], T.GB[:], 0.0, AO.mult, AO.add)
-        V("QS", "DF", "tt", T.DF[:], T.QS[:, 164:320:5], T.QS[:, 4:160:5], AO.subtract)
+        V("KEEP5 QB0 QB1 QB2 QB3 QB4 QB5", "QS", "scan", T.QS[:], T.KEEP5[:], T.QB[:], 0.0, AO.mult, AO.add)
         V("PG " + OPA, "UB", "tt", T.UB[:], T.PG[:], T.OPN[:, 0:80], AO.mult)
-        V("DF QS", "DG", "tt", T.DG[:], T.DF[:], T.QS[:, 324:480:5], AO.mult)
-        V(KKA, "KM", "ts", T.KM[:], T.KK[:], -32.0, None, AO.add)
-        V("DG QS", "RS", "tt", T.RS[:], T.DG[:], T.QS[:, 4:160:5], AO.add)
-        V("Q0 TR", "Q1", "tt", T.Q1[:], T.Q0[:], T.TR[:], AO.mult)
+        V("QS", "DF", "tt", T.DF[:], T.QS[:, 163:320:5], T.QS[:, 3:160:5], AO.subtract)
+        V("UB H16", "KU", "tt", T.KU[:], T.UB[:], T.H16[:, 1:81], AO.mult)
+        V("DF QS", "DG", "tt", T.DG[:], T.DF[:], T.QS[:, 323:480:5], AO.mult)
+        V("KU", "LC0", "tc", T.LC[:, 0:16], T.KU[:, 0::5])
+        V("DG QS", "RS", "tt", T.RS[:], T.DG[:], T.QS[:, 3:160:5], AO.add)
+        V("KU", "LC1", "tc", T.LC[:, 16:32], T.KU[:, 1::5])
         V("RS", "LKD", "tc", T.LKD[:], T.RS[:, 16:32])
         V("RS XL", "LJA", "tt", T.LJA[:], T.RS[:, 0:16], T.XL[:], AO.add)
-        S("OHW LKD", "OHD", T.OHD[:], T.OHW[:, 0:48].indirect(T.LKD[:, 0:16]), AF.Copy)
-        V("KM UB", "KU", "tt", T.KU[:], T.KM[:], T.UB[:], AO.mult)
+        S("OHW LKD", "OHD", T.OHD[:], T.OHW[:, 0:32].indirect(T.LKD[:, 0:16]), AF.Copy)
+        V("KU", "LC2", "tc", T.LC[:, 32:48], T.KU[:, 2::5])
         V("LJA", "LJD", "tc", T.LJD[:], T.LJA[:])
-        V("OHD LJD " + NHA, "SEL", "tt", T.SEL[:], T.NHF[:, 0:1024].indirect(T.LJD[:, 0:16]), T.OHD[:], AO.mult)
-        mms("BO SEL", "AUX0", [(T.AUX0[:, 0:256], T.BO[:], T.SEL[:], True, True)])
-        for s in range(4):
-            V("KU", "LC", "ts", T.LC[:, 16 * s:16 * s + 16], T.KU[:, s::5], 32.0, None, AO.add)
-        V("Q1 " + LSA, "Q2", "tt", T.Q2[:], T.Q1[:], T.LST[:], AO.add)
+        V("KU", "LC3", "tc", T.LC[:, 48:64], T.KU[:, 3::5])
+        S("OHW LC0 LC1 LC2 LC3", "OHM", T.OHM[:], T.OHW[:, 0:32].indirect(T.LC[:, 0:64]), AF.Copy)
         if t < 2:
             V(OPA, "ZR", "red", T.ZR[:, 0:1], T.OPN[:, 4:80:5], AxisListType.X, AO.add)
+        V("OHD LJD " + NHA, "SEL", "tt", T.SEL[:], T.NHF[:, 0:1024].indirect(T.LJD[:, 0:16]), T.OHD[:], AO.mult)
+        mms("BO SEL", "AUX0", [(T.AUX0[:, 0:256], T.BO[:], T.SEL[:], True, True)])
+        if t < 2:
             mms("ONE ZR", "AUX1", [(T.AUX1[:, 0:1], T.ONE[:], T.ZR[:, 0:1], True, True)])
-        V("Q2", "SL", "tc", T.SL[:], T.Q2[:])
+        V("OHC LC0 LC1 LC2 LC3 " + NHA, "NP", "tt", T.NP[:], T.OHC[:, 0:32].indirect(T.LC[:, 0:64]), T.NHF[:], AO.mult)
         for s in range(4):
-            V("AUX0 " + NHA, "DL", "tt", T.DL[:, 256 * s:256 * s + 256], T.AUX0[:, 0:256], T.NHF[:, 256 * s:256 * s + 256], AO.subtract)
-        V("OHW LC DL", "BB", "tt", T.BB[:], T.OHW[:, 0:48].indirect(T.LC[:, 0:64]), T.DL[:], AO.mult)
+            V("AUX0 OHM", "BB%d" % s, "tt", T.BB[:, 256 * s:256 * s + 256], T.AUX0[:, 0:256], T.OHM[:, 256 * s:256 * s + 256], AO.mult)
         if t == 0:
             V("AUX1", "ZA", "tc", T.ZA[:, 0:1], T.AUX1[:, 0:1])
         elif t == 1:
             V("AUX1 ZA", "ZA", "tt", T.ZA[:, 0:1], T.AUX1[:, 0:1], T.ZA[:, 0:1], AO.add)
-        V(NHA + " BB SL", PFA, "tt", T.PF[:, 0:5136].indirect(T.SL[:, 0:64]), T.NHF[:], T.BB[:], AO.add)
+        V("NP BB0 BB1 BB2 BB3 SL", PFA, "tt", T.PF[:, 0:5136].indirect(T.SL[:, 0:64]), T.NP[:], T.BB[:], AO.add)
     for q in range(4):
         c0, c1, k = 512 * q, 512 * q + 512, str(q)
         S("PFH" + k, "HP" + k, T["HP" + k][:], T.PF[:, 2049 + c0:2049 + c1], AF.Copy, scale=4096.0)
@@ -340,13 +443,3 @@ def rank_program(g, core, T, topo):
     need("G", "ls", cnt["ls"])
     for sem in ("aS1", "aS2", "aF1", "aF2"):
         need("G", sem, narr)
-
-
-def opn(T, s):
-    return T.OPN[:, s:80:5]
-
-
-def unpack_lo(V, T, q):
-    c0, c1, k = 512 * q, 512 * q + 512, str(q)
-    V("PFT PK%d HP%s" % (q // 2, k), "PFL" + k, "tt", T.PF[:, 1 + c0:1 + c1], T["HP" + k][:], T.PK[:, c0:c1], AO.subtract) if False else \
-        V("PFT PK%d HP%s" % (q // 2, k), "PFL" + k, "tt", T.PF[:, 1 + c0:1 + c1], T.PK[:, c0:c1], T["HP" + k][:], AO.subtract)

@@ -22,17 +22,17 @@ for _n, _c, _d in [
         ("ST0", 288, F32), ("ST1", 288, F32), ("ST2", 288, F32),
         ("FS", 4096, BF), ("WW", 8192, BF), ("A3", [16, 256], BF),
         ("NU", 1024, U16), ("NHF", 1024, F32), ("NP", 1024, F32), ("OHM", 1024, F32), ("BB", 1024, F32), ("SEL", 256, F32), ("OHD", 256, F32),
-        ("SC", 256, F32), ("KH", 80, I32), ("HK", 96, I32), ("OPN", 96, F32), ("LST", 64, F32),
-        ("CCH", 48, I32), ("OX", 16, F32), ("OXT", 16, F32), ("XLW", 16, F32),
-        ("T0", 16, F32), ("T1", 16, F32), ("T2", 16, F32), ("T3", 16, F32), ("FA", 16, I32),
-        ("FL", 16, U16), ("LUH", 64, U16), ("DP", 80, I32), ("AS", 80, I32), ("OD", 80, I32), ("CLB", 80, F32),
+        ("SC", 1024, I32), ("KF", 16, I32), ("HK", 96, I32), ("OPN", 96, F32), ("LST", 64, F32),
+        ("CI", 128, I32), ("LW", 160, U16), ("OX", 16, F32), ("OXT", 16, F32), ("XLW", 16, F32),
+        ("T0", 16, F32), ("T1", 16, F32), ("T2", 16, F32), ("T3", 16, F32),
+        ("DP", 80, I32), ("AS", 80, I32), ("OD", 80, I32), ("CLB", 80, F32),
         ("KSS", 80, F32), ("H16", 96, F32), ("EQB", 80, F32), ("GB", 80, F32), ("PG", 80, F32), ("UB", 80, F32),
-        ("QB", 480, F32), ("QS", 480, F32), ("DF", 32, F32), ("DG", 32, F32), ("RS", 32, F32), ("LJA", 16, F32), ("LJD", 16, U16), ("LKD", 16, U16),
+        ("QB", 400, F32), ("QS", 400, F32), ("DF", 32, F32), ("DG", 32, F32), ("RS", 32, F32), ("LJA", 16, F32), ("LJD", 16, U16), ("LKD", 16, U16),
         ("KU", 80, F32), ("LC", 64, U16), ("Q0", 64, F32), ("Q1", 64, F32), ("Q2", 64, F32), ("SL", 64, U16),
         ("ZR", 1, F32), ("ZA", 1, F32),
         ("IM", 160, F32), ("IG", 128, F32), ("IPI", 2, I32), ("IQI", 2, I32), ("IGI", 2, I32), ("CF", 4, F32),
         ("IDN", 128, F32), ("WB", 144, BF), ("BO", 128, F32), ("ONE", 128, F32), ("L8", 128, BF), ("MG", 8, F32), ("E16", 16, F32),
-        ("OHW", 32, F32), ("OHC", 32, F32), ("KEEP", 768, BF), ("RST", 128, F32), ("KEEP5", 480, F32), ("XRI", 128, I32), ("XREP", 128, U16),
+        ("OHW", 32, F32), ("OHC", 32, F32), ("KEEP", 768, BF), ("RST", 128, F32), ("KEEP5", 400, F32), ("XRI", 128, I32), ("XREP", 128, U16),
         ("IA", 16, F32), ("XL", 16, F32), ("TRI", 64, F32), ("TR", 64, F32), ("SI", 80, F32), ("PLC", 256, F32),
         ("QK", 256, F32), ("XZ", 256, F32), ("XA", 256, F32), ("XB", 256, F32), ("XC", 256, F32)]:
     _s(_n, _c, _d)
@@ -143,7 +143,7 @@ def rank_program(g, core, T, topo):
     iota("HK", [[0, 96]], 0, 0)
     iota("TRI", [[256, 4], [16, 16]], 4097, 0)
     iota("SI", [[0, 16], [256, 5]], 0, 0)
-    iota("KEEP5", [[0, 480]], 1, 0)
+    iota("KEEP5", [[0, 400]], 1, 0)
     iota("ONE", [[0, 128]], 1, 0)
     iota("AS", [[0, 80]], 0, 0)
     iota("EQB", [[0, 80]], 0, 0)
@@ -221,7 +221,7 @@ def rank_program(g, core, T, topo):
         return T.WW[:, 4096 * X:4096 * X + 4096]
 
     def lists_of_visit(t):
-        V("ST%d" % t, "LU01 LU11", "tc", T.LUH[:, 0:16], T["ST%d" % t][:, 256:272])
+        V("ST%d" % t, "LU01 LU11", "tc", T.LW[:, 8:24], T["ST%d" % t][:, 256:272])
 
     unpack_lo(0)
     unpack_hi(2)
@@ -236,8 +236,8 @@ def rank_program(g, core, T, topo):
         fo, fok = T["FO%d" % t], "FO%d" % t
 
         def pf(X, s):
-            c0 = 256 * s - 256 + 128 * X
-            V("%s LU%d%d" % (PFA, X, s), "NU%d%d" % (X, s), "tc", T.NU[:, c0:c0 + 128], T.PF[:, 0:4112].indirect(T.LUH[:, 16 * s - 16 + 8 * X:16 * s - 8 + 8 * X]))
+            c0, l0 = 256 * s - 256 + 128 * X, 32 * s - 24 + 8 * X
+            V("%s LU%d%d" % (PFA, X, s), "NU%d%d" % (X, s), "tc", T.NU[:, c0:c0 + 128], T.PF[:, 0:4112].indirect(T.LW[:, l0:l0 + 8]))
 
         def pay(X):
             mms("IDN " + stk, "KEY%d" % X, [(T["KEY%d" % X][:, 0:128], T.IDN[:], st[:, 128 * X:128 * X + 128], True, False)])
@@ -264,33 +264,46 @@ def rank_program(g, core, T, topo):
                 T.A3[:, 8 * X + a0:8 * X + a1, 16 * b:16 * b + 16], False, i == len(CH) - 1 and b == 15) for b in range(16)])
 
         def nh(s):
-            S("%s LU0%d LU1%d" % (PFA, s, s), "NH%d" % s, T.NHF[:, 256 * s - 256:256 * s], T.PF[:, 0:4112].indirect(T.LUH[:, 16 * s - 16:16 * s]), AF.Copy)
+            S("%s LU0%d LU1%d" % (PFA, s, s), "NH%d" % s, T.NHF[:, 256 * s - 256:256 * s], T.PF[:, 0:4112].indirect(T.LW[:, 32 * s - 24:32 * s - 8]), AF.Copy)
 
-        def choose(X, s, fill=()):
-            k = "%d%d" % (X, s)
-            c16 = slice(16 * s - 16 + 8 * X, 16 * s - 8 + 8 * X)
-            fill = list(fill)
-            h = (len(fill) + 1) // 2
-            V("RST KEY%d" % X, "SC%d" % X, "scan", T.SC[:, 128 * X:128 * X + 128], T.RST[:], T["KEY%d" % X][:, 0:128], 0.0, AO.add, AO.min)
-            for f in fill[:h]:
+        def choose(X, s, fill=(), last=()):
+            k, c0, i0 = "%d%d" % (X, s), 256 * s - 256 + 128 * X, 32 * s - 32
+            fa, cc = (i0, i0 + 8) if X == 0 else (i0 + 24, i0 + 16)
+            key, fill, last = T.SC[:, c0 + 15:c0 + 128:16], list(fill), list(last)
+
+            def some(n):
+                while len(fill) > n:
+                    fill.pop(0)()
+            V("RST KEY%d" % X, "SC" + k, "scan", T.SC[:, c0:c0 + 128], T.RST[:], T["KEY%d" % X][:, 0:128], 0.0, AO.add, AO.min)
+            mixed = len(fill) >= 3
+            some(3 if len(fill) > 3 else 2 if mixed else 0)
+            V("SC" + k, "HK" + k, "ts", a5(T.HK, X, s), key, 13, 15, AO.arith_shift_right, AO.bitwise_and)
+            some(2)
+            if s < 4:
+                V("SC" + k, "CC" + k, "ts", T.CI[:, cc:cc + 8], key, 8191, None, AO.bitwise_and)
+            some(1)
+            for f in last[:1]:
                 f()
-            V("SC%d" % X, "KH" + k, "tc", a5(T.KH, X, s), T.SC[:, 128 * X + 15:128 * X + 128:16])
-            for f in fill[h:]:
+            if mixed:
+                if s < 4:
+                    V("CC" + k, "LU%d%d" % (X, s + 1), "tc", T.LW[:, 32 + cc:40 + cc], T.CI[:, cc:cc + 8])
+                some(0)
+                if s < 4:
+                    pf(X, s + 1)
+            V("OX HK" + k, "FA" + k, "tt", T.CI[:, fa:fa + 8], a5(T.HK, X, s), T.OX[:, 8 * X:8 * X + 8], AO.add)
+            if s < 4 and not mixed:
+                V("CC" + k, "LU%d%d" % (X, s + 1), "tc", T.LW[:, 32 + cc:40 + cc], T.CI[:, cc:cc + 8])
+            for f in last[1:]:
                 f()
-            V("KH" + k, "HK" + k, "ts", a5(T.HK, X, s), a5(T.KH, X, s), 13, 15, AO.arith_shift_right, AO.bitwise_and)
+            V("FA" + k, "FL%d" % X, "tc", T.LW[:, 32 + fa:40 + fa], T.CI[:, fa:fa + 8])
+            rd, fl = "FL%d WF%dv WF%da WF%db WD%d0 WD%d1" % (X, X, X, X, X, X), T.LW[:, 32 + fa:40 + fa]
             if s < 4:
-                V("KH" + k, "CC" + k, "ts", T.CCH[:, c16], a5(T.KH, X, s), 8191, None, AO.bitwise_and)
-            V("OX HK" + k, "FA%d" % X, "tt", T.FA[:, 8 * X:8 * X + 8], a5(T.HK, X, s), T.OX[:, 8 * X:8 * X + 8], AO.add)
-            if s < 4:
-                V("CC" + k, "LU%d%d" % (X, s + 1), "tc", T.LUH[:, 16 * s + 8 * X:16 * s + 8 * X + 8], T.CCH[:, c16])
-            V("FA%d" % X, "FL%d" % X, "tc", T.FL[:, 8 * X:8 * X + 8], T.FA[:, 8 * X:8 * X + 8])
-            rd = "FL%d WF%dv WF%da WF%db WD%d0 WD%d1" % (X, X, X, X, X, X)
-            if s < 4:
-                S(rd, "FS%d" % X, T.FS[:, 2048 * X:2048 * X + 2048:16], win(X).indirect(T.FL[:, 8 * X:8 * X + 8]), AF.Abs)
-                pf(X, s + 1)
+                S(rd, "FS%d" % X, T.FS[:, 2048 * X:2048 * X + 2048:16], win(X).indirect(fl), AF.Abs)
+                if not mixed:
+                    pf(X, s + 1)
                 pay(X)
             else:
-                S(rd, fok, fo[:, 128 * X:128 * X + 128], win(X).indirect(T.FL[:, 8 * X:8 * X + 8]), AF.Abs)
+                S(rd, fok, fo[:, 128 * X:128 * X + 128], win(X).indirect(fl), AF.Abs)
 
         def keep(s):
             H = [T.HK[:, j:80:5] for j in range(5)]
@@ -325,8 +338,9 @@ def rank_program(g, core, T, topo):
                     mul(opn(4), t0, t2, "OPN4", "T0", "T2")
             if s < 4:
                 later("OPN%d" % s, "OXT", "ts", T.OXT[:], opn(s), 2048.0, None, AO.mult)
-                later("CC0%d CC1%d OPN%d" % (s, s, s), "LST%d" % (s + 1), "tt", T.LST[:, 16 * s:16 * s + 16], T.CCH[:, 16 * s - 16:16 * s], opn(s), AO.mult)
                 later("OXT XLW", "OX", "tt", T.OX[:], T.OXT[:], T.XLW[:], AO.add)
+                later("CC0%d CC1%d OPN%d" % (s, s, s), "LST%d" % (s + 1), "tt", T.LST[:, 16 * s:16 * s + 16], T.CI[:, 32 * s - 24:32 * s - 8], opn(s), AO.mult)
+            later("SC0%d SC1%d" % (s, s), "DP%d" % s, "ts", T.DP[:, s:80:5], T.SC[:, 256 * s - 241:256 * s:16], 17, 1, AO.arith_shift_right, AO.bitwise_and)
             return todo
 
         pay(0)
@@ -337,17 +351,25 @@ def rank_program(g, core, T, topo):
         fe(0, "a")
         fe(0, "b")
         fe(1, "a")
-        pf(0, 1)
+        spare = []
         for s in range(1, 5):
             for X in range(2):
                 fe(X, "v")
+                if s == 1 and X == 0:
+                    pf(0, 1)
+                    pf(1, 1)
+                elif s == 1:
+                    V(stk, "LST1", "tc", T.LST[:, 0:16], st[:, 256:272])
+                elif spare:
+                    spare.pop()()
                 gather(X, 0, s)
                 dist(X, 0)
-                if X == 1:
-                    choose(0, s, keep(s - 1) if s > 1 else ())
-                    if s < 4:
-                        fe(0, "a")
-                elif s > 1:
+                if X == 1 and s < 4:
+                    k2 = keep(s - 1) if s > 1 else []
+                    choose(0, s, k2[:-2])
+                    spare.extend(k2[-2:])
+                    fe(0, "a")
+                elif X == 0 and s > 1:
                     choose(1, s - 1)
                     fe(1, "a")
                 gather(X, 1, s)
@@ -355,39 +377,40 @@ def rank_program(g, core, T, topo):
                 if X == 0 or s < 4:
                     fe(1 - X, "b")
                 if X == 0 and s == 1:
-                    pf(1, 1)
-                    V(stk, "LST1", "tc", T.LST[:, 0:16], st[:, 256:272])
+                    V("AUX1", "KF", "tc", T.KF[:], T.AUX1[:, 0:16])
                     V("HK " + stk, "HK00 HK10", "tc", T.HK[:, 0:80:5], st[:, 272:288])
                     V("XLW", "OX", "ts", T.OX[:], T.XLW[:], 2048.0, None, AO.add)
-                    V("AUX1", "KH0", "tc", T.KH[:, 0:80:5], T.AUX1[:, 0:16])
+                    V("KF", "DP0", "ts", T.DP[:, 0:80:5], T.KF[:], 17, 1, AO.arith_shift_right, AO.bitwise_and)
                 if X == 1:
                     nh(s)
+        k3 = keep(3)
+        choose(0, 4, k3[:-2])
         if t == 0:
             late_constants()
-        if t < 2:
-            lists_of_visit(t + 1)
+        for f in spare + k3[-2:]:
+            f()
         LSA = "LST1 LST2 LST3 LST4"
-        V(LSA, "Q0", "ts", T.Q0[:], T.LST[:], 0.0, None, AO.is_equal)
-        V("Q0 TR", "Q1", "tt", T.Q1[:], T.Q0[:], T.TR[:], AO.mult)
-        V("Q1 " + LSA, "Q2", "tt", T.Q2[:], T.Q1[:], T.LST[:], AO.add)
-        V("Q2", "SL", "tc", T.SL[:], T.Q2[:])
-        choose(1, 4)
+        choose(1, 4, [lambda: V(LSA, "Q0", "ts", T.Q0[:], T.LST[:], 0.0, None, AO.is_equal)],
+               [lambda: V("Q0 TR", "Q1", "tt", T.Q1[:], T.Q0[:], T.TR[:], AO.mult),
+                lambda: V("Q1 " + LSA, "Q2", "tt", T.Q2[:], T.Q1[:], T.LST[:], AO.add)])
         if t < 2:
             send((rank + 1) % nrank, fo[:], T["FIN%d" % (t + 1)][:], "aF%d" % (t + 1), fok)
         else:
             dma("Y", fok, "yf", T.yf[:], fo[:])
-        KHA = "KH0 " + " ".join("KH%d%d" % (X, s) for X in range(2) for s in range(1, 5))
         HKA = "HK " + " ".join("HK%d%d" % (X, s) for X in range(2) for s in range(5))
         OPA, NHA = "OPN OPN1 OPN2 OPN3 OPN4", "NH1 NH2 NH3 NH4"
-        Q = [T.QB[:, 80 * i:80 * i + 80] for i in range(6)]
+        Q = [T.QB[:, 80 * i:80 * i + 80] for i in range(5)]
         k4 = keep(4)
         for f in k4[:6]:
             f()
+        V("Q2", "SL", "tc", T.SL[:], T.Q2[:])
         V(HKA, "H16", "ts", T.H16[:, 0:81], T.HK[:, 0:81], 16.0, None, AO.add)
         k4[6]()
-        V(KHA, "DP", "ts", T.DP[:], T.KH[:], 17, 1, AO.arith_shift_right, AO.bitwise_and)
+        k4[8]()
+        if t < 2:
+            lists_of_visit(t + 1)
         k4[7]()
-        V("DP AS", "AS", "tt", T.AS[:, 0:79], T.DP[:, 0:79], T.DP[:, 1:80], AO.add)
+        V("DP0 DP1 DP2 DP3 DP4 AS", "AS", "tt", T.AS[:, 0:79], T.DP[:, 0:79], T.DP[:, 1:80], AO.add)
         V(OPA, "CLB", "tt", T.CLB[:], T.OPN[:, 0:80], T.OPN[:, 1:81], AO.subtract)
         if t > 0:
             V("AS ZA", "AS", "ts", T.AS[:], T.AS[:], T.ZA[:, 0:1], None, AO.add)
@@ -397,19 +420,21 @@ def rank_program(g, core, T, topo):
         V("AS", "OD", "ts", T.OD[:], T.AS[:], 1, None, AO.bitwise_and)
         for j in range(4):
             V("H16 KSS EQB", "EQ%d" % j, "tt", T.EQB[:, j::5], T.H16[:, j:80:5], T.KSS[:, 3::5], AO.is_equal)
+        if t < 2:
+            V(OPA, "ZR", "red", T.ZR[:, 0:1], T.OPN[:, 4:80:5], AxisListType.X, AO.add)
         V("EQB EQ0 EQ1 EQ2 EQ3 " + OPA, "GB", "tt", T.GB[:], T.EQB[:], T.OPN[:, 0:80], AO.mult)
         V("GB SI", "QB0", "tt", Q[0], T.GB[:], T.SI[:], AO.mult)
         V("GB H16", "QB1", "tt", Q[1], T.GB[:], T.H16[:, 1:81], AO.mult)
         V("GB OD", "QB4", "tt", Q[4], T.GB[:], T.OD[:], AO.mult)
-        V("GB OD", "QB5", "tt", Q[5], T.GB[:], T.OD[:], AO.mult)
         V("KEEP5 GB", "PG", "scan", T.PG[:], T.KEEP5[:, 0:80], T.GB[:], 0.0, AO.mult, AO.add)
-        V("KEEP5 QB0 QB1 QB2 QB3 QB4 QB5", "QS", "scan", T.QS[:], T.KEEP5[:], T.QB[:], 0.0, AO.mult, AO.add)
+        V("KEEP5 QB0 QB1 QB2 QB3 QB4", "QS", "scan", T.QS[:], T.KEEP5[:], T.QB[:], 0.0, AO.mult, AO.add)
         V("PG " + OPA, "UB", "tt", T.UB[:], T.PG[:], T.OPN[:, 0:80], AO.mult)
         V("QS", "DF", "tt", T.DF[:], T.QS[:, 163:320:5], T.QS[:, 3:160:5], AO.subtract)
         V("UB H16", "KU", "tt", T.KU[:], T.UB[:], T.H16[:, 1:81], AO.mult)
-        V("DF QS", "DG", "tt", T.DG[:], T.DF[:], T.QS[:, 323:480:5], AO.mult)
+        V("DF QS", "DG1", "tt", T.DG[:, 16:32], T.DF[:, 16:32], T.QS[:, 323:400:5], AO.mult)
+        V("DF QS", "DG0", "tt", T.DG[:, 0:16], T.DF[:, 0:16], T.QS[:, 323:400:5], AO.mult)
         V("KU", "LC0", "tc", T.LC[:, 0:16], T.KU[:, 0::5])
-        V("DG QS", "RS", "tt", T.RS[:], T.DG[:], T.QS[:, 3:160:5], AO.add)
+        V("DG0 DG1 QS", "RS", "tt", T.RS[:], T.DG[:], T.QS[:, 3:160:5], AO.add)
         V("KU", "LC1", "tc", T.LC[:, 16:32], T.KU[:, 1::5])
         V("RS", "LKD", "tc", T.LKD[:], T.RS[:, 16:32])
         V("RS XL", "LJA", "tt", T.LJA[:], T.RS[:, 0:16], T.XL[:], AO.add)
@@ -418,8 +443,6 @@ def rank_program(g, core, T, topo):
         V("LJA", "LJD", "tc", T.LJD[:], T.LJA[:])
         V("KU", "LC3", "tc", T.LC[:, 48:64], T.KU[:, 3::5])
         S("OHW LC0 LC1 LC2 LC3", "OHM", T.OHM[:], T.OHW[:, 0:32].indirect(T.LC[:, 0:64]), AF.Copy)
-        if t < 2:
-            V(OPA, "ZR", "red", T.ZR[:, 0:1], T.OPN[:, 4:80:5], AxisListType.X, AO.add)
         V("OHD LJD " + NHA, "SEL", "tt", T.SEL[:], T.NHF[:, 0:1024].indirect(T.LJD[:, 0:16]), T.OHD[:], AO.mult)
         mms("BO SEL", "AUX0", [(T.AUX0[:, 0:256], T.BO[:], T.SEL[:], True, True)])
         if t < 2:

from concourse.mybir import dt, AluOpType, AxisListType, ActivationFunctionType
import comms_topo

AO = AluOpType
AF = ActivationFunctionType
CH = [(0, 5), (5, 8)]
FE = {"v": (0, 3), "a": (3, 5), "b": (5, 8)}

F32, BF, I32, U16 = "float32", "bfloat16", "int32", "uint16"
SCRATCH = {}


def _s(name, cols, dtype, where="sbuf"):
    SCRATCH[name] = (where, [128] + (cols if isinstance(cols, list) else [cols]), dtype)


for _n, _c, _d in [
        ("R", 4096, BF), ("PF", 5136, F32), ("PK", 2048, I32), ("TI", 2048, I32), ("YO", 2048, F32),
        ("JI", [16, 16], I32), ("JF", [16, 16], F32), ("JT", [16, 128], F32), ("SRI", 256, I32), ("SRB", 256, BF),
        ("SRG", 256, BF), ("FX0", 256, BF), ("FIN1", 256, BF), ("FIN2", 256, BF),
        ("FO0", 256, BF), ("FO1", 256, BF), ("FO2", 256, BF),
        ("ST0", 288, F32), ("ST1", 288, F32), ("ST2", 288, F32),
        ("FS", 4096, BF), ("WW", 8192, BF), ("A3", [16, 256], BF),
        ("NU", 1024, U16), ("NHF", 1024, F32), ("NP", 1024, F32), ("OHM", 1024, F32), ("BB", 1024, F32), ("SEL", 256, F32), ("OHD", 256, F32),
        ("SC", 1024, I32), ("KF", 16, I32), ("HK", 96, I32), ("OPN", 96, F32), ("LST", 64, F32),
        ("CI", 128, I32), ("LW", 160, U16), ("OX", 16, F32), ("OXT", 16, F32), ("XLW", 16, F32),
        ("T0", 16, F32), ("T1", 16, F32), ("T2", 16, F32), ("T3", 16, F32),
        ("DP", 80, I32), ("AS", 80, I32), ("OD", 80, I32), ("CLB", 80, F32),
        ("KSS", 80, F32), ("H16", 96, F32), ("EQB", 80, F32), ("GB", 80, F32), ("PG", 80, F32), ("UB", 80, F32),
        ("QB", 400, F32), ("QS", 400, F32), ("DF", 32, F32), ("DG", 32, F32), ("RS", 32, F32), ("LJA", 16, F32), ("LJD", 16, U16), ("LKD", 16, U16),
        ("KU", 80, F32), ("LC", 64, U16), ("Q0", 64, F32), ("Q1", 64, F32), ("Q2", 64, F32), ("SL", 64, U16),
        ("ZR", 1, F32), ("ZA", 1, F32),
        ("IM", 160, F32), ("IG", 128, F32), ("IPI", 2, I32), ("IQI", 2, I32), ("IGI", 2, I32), ("CF", 4, F32),
        ("IDN", 128, F32), ("WB", 144, BF), ("BO", 128, F32), ("ONE", 128, F32), ("L8", 128, BF), ("MG", 8, F32), ("E16", 16, F32),
        ("OHW", 32, F32), ("OHC", 32, F32), ("KEEP", 768, BF), ("RST", 128, F32), ("KEEP5", 400, F32), ("XRI", 128, I32), ("XREP", 128, U16),
        ("IA", 16, F32), ("XL", 16, F32), ("TRI", 64, F32), ("TR", 64, F32), ("SI", 80, F32), ("PLC", 256, F32),
        ("QK", 256, F32), ("XZ", 256, F32), ("XA", 256, F32), ("XB", 256, F32), ("XC", 256, F32)]:
    _s(_n, _c, _d)
for _n in ["KEY0", "KEY1", "AUX0", "AUX1", "HP0", "HP1", "HP2", "HP3"]:
    _s(_n, 512, F32, "psum")

SEMAPHORES = ["sv", "ss", "sp", "sg", "aS1", "aS2", "aF1", "aF2", "ls"] + ["d%d" % i for i in range(12)]


def rank_program(g, core, T, topo):
    rank = T.rank_of(core)
    if rank is None:
        return
    nrank = len(T.cores)
    ENG = {"V": (g.vector, "sv"), "S": (g.scalar, "ss"), "P": (g.tensor, "sp"), "G": (g, "sg"), "Y": (g.sync, None)}
    cnt = {s: 0 for s in SEMAPHORES}
    waited, Wr, Rd, ndma = {}, {}, {}, [0]

    def need(e, sem, val):
        if waited.get((e, sem), 0) < val:
            ENG[e][0].wait_ge(T.sem[sem], val)
            waited[(e, sem)] = val

    def sync(e, reads, writes):
        own, todo = ENG[e][1], {}
        for k in reads:
            for s, v in Wr.get(k, {}).items():
                todo[s] = max(todo.get(s, 0), v)
        for k in writes:
            for s, v in Wr.get(k, {}).items():
                todo[s] = max(todo.get(s, 0), v)
            for s, v in Rd.get(k, {}).items():
                if s != own:
                    todo[s] = max(todo.get(s, 0), v)
        for s, v in todo.items():
            need(e, s, v)

    def note(sem, val, reads, writes):
        for k in reads:
            Rd.setdefault(k, {})[sem] = val
        for k in writes:
            Wr.setdefault(k, {})[sem] = val

    def run(e, reads, writes, name, *a, **kw):
        reads, writes = reads.split(), writes.split()
        sync(e, reads, writes)
        q, sem = ENG[e]
        ins = {"tc": lambda: q.tensor_copy(*a, **kw), "tt": lambda: q.tensor_tensor(*a, **kw), "ts": lambda: q.tensor_scalar(*a, **kw),
               "scan": lambda: q.tensor_tensor_scan(*a, **kw), "memset": lambda: q.memset(*a, **kw), "red": lambda: q.tensor_reduce(*a, **kw),
               "act": lambda: q.activation(*a, **kw), "mm": lambda: q.matmul(*a, **kw), "iota": lambda: q.iota(*a, **kw)}[name]()
        cnt[sem] += 1
        ins.then_inc(T.sem[sem], 1)
        note(sem, cnt[sem], reads, writes)

    def V(reads, writes, name, *a, **kw):
        run("V", reads, writes, name, *a, **kw)

    def S(reads, writes, out, in_, func, **kw):
        run("S", reads, writes, "act", out, in_, func, **kw)

    def mms(reads, writes, calls):
        sync("P", reads.split(), writes.split())
        for c in calls[:-1]:
            g.tensor.matmul(*c)
        run("P", reads, writes, "mm", *calls[-1])

    def dma(e, reads, writes, out, in_):
        reads, writes = reads.split(), writes.split()
        sync(e, reads, writes)
        sem = "d%d" % ndma[0]
        ndma[0] += 1
        ENG[e][0].dma_start(out, in_).then_inc(T.sem[sem], 16)
        cnt[sem] = 16
        note(sem, 16, reads, writes)

    def send(dst_rank, src, dst, arr, key):
        d = T.cores[dst_rank]
        rid, pid, _ = topo.addr(d)
        sync("G", [key], [])
        g.remote_dma(out_ap=dst, in_ap=src, remote_sem=T.sem[arr], local_sem=T.sem["ls"], pid=pid, routing_id=rid,
                     dma_engine_mask=topo.mask(core, d))
        cnt["ls"] += len(topo.engines(core, d))

    narr = len(topo.engines(core, T.cores[(rank + 1) % nrank]))

    dma("Y", "", "JI", T.JI[:, :, :], T.jc[:])
    dma("S", "", "SRI", T.SRI[0:8, :], T.sr[:])
    dma("Y", "", "PK0", T.PK[:, 0:1024], T.pk[:, 0:1024])
    dma("S", "", "FX0", T.FX0[:], T.fx[:])
    dma("Y", "", "PK1", T.PK[:, 1024:2048], T.pk[:, 1024:2048])
    dma("Y", "", "R", T.R[:], T.rt[:])

    def iota(name, pat, base, cm, key=None):
        run("G", "", key or name, "iota", T[name][:], pat, base, cm,
            **({} if SCRATCH[name][2] == I32 else {"allow_small_or_imprecise_dtypes": True}))
    iota("IPI", [[0, 2]], 0, 1)
    iota("IM", [[1, 160]], 0, 0)
    iota("IG", [[1, 8], [0, 16]], 0, 0)
    iota("XZ", [[0, 256]], 0, 0)
    iota("KEEP", [[0, 768]], 1, 0)
    iota("QK", [[0, 16], [1, 16]], 0, 0)
    iota("PLC", [[0, 16], [8192, 16]], -16777215, 0)
    iota("XRI", [[16, 128]], 0, 0)
    iota("IA", [[16, 16]], 0, 0)
    iota("RST", [[0, 128]], 0, 0)
    iota("FS", [[0, 4096]], 0, 0, "FS0 FS1")
    iota("OPN", [[0, 96]], 1, 0)
    iota("HK", [[0, 96]], 0, 0)
    iota("TRI", [[256, 4], [16, 16]], 4097, 0)
    iota("SI", [[0, 16], [256, 5]], 0, 0)
    iota("KEEP5", [[0, 400]], 1, 0)
    iota("ONE", [[0, 128]], 1, 0)
    iota("AS", [[0, 80]], 0, 0)
    iota("EQB", [[0, 80]], 0, 0)
    iota("OHW", [[0, 32]], 0, 0)
    iota("OHC", [[0, 32]], 1, 0)
    V("IPI", "IQI", "ts", T.IQI[:], T.IPI[:], 15, None, AO.bitwise_and)
    V("IPI", "IGI", "ts", T.IGI[:], T.IPI[:], 4, None, AO.arith_shift_right)
    V("IPI", "CF0", "tc", T.CF[:, 0:1], T.IPI[:, 0:1])
    V("IQI", "CF1", "tc", T.CF[:, 1:2], T.IQI[:, 0:1])
    V("IGI", "CF2", "tc", T.CF[:, 2:3], T.IGI[:, 0:1])
    V("IGI", "CF3", "ts", T.CF[:, 3:4], T.IGI[:, 0:1], 16.0, 15.0, AO.mult, AO.add)
    p_c, q_c, g_c, e_c = [T.CF[:, i:i + 1] for i in range(4)]
    V("IM CF2", "MG", "ts", T.MG[:], T.IM[:, 0:8], g_c, None, AO.is_equal)
    V("IM CF3", "WB", "ts", T.WB[:, 0:143], T.IM[:, 0:143], e_c, 131072.0, AO.is_equal, AO.mult)
    V("IM CF1", "E16", "ts", T.E16[:], T.IM[:, 0:16], q_c, None, AO.is_equal)
    V("IG CF0", "L8", "ts", T.L8[0:8, :], T.IG[0:8, :], T.CF[0:8, 0:1], None, AO.is_equal)
    V("IM CF0", "IDN", "ts", T.IDN[:], T.IM[:, 0:128], p_c, None, AO.is_equal)

    def late_constants():
        V("IG CF2", "BO", "ts", T.BO[:], T.IG[:], g_c, None, AO.is_equal)
        V("IM CF1", "OHW", "ts", T.OHW[:, 16:32], T.IM[:, 0:16], q_c, None, AO.is_equal)
        V("IM CF1", "OHC", "ts", T.OHC[:, 16:32], T.IM[:, 0:16], q_c, None, AO.not_equal)
        V("TRI CF1", "TR", "ts", T.TR[:], T.TRI[:], q_c, None, AO.add)
        V("", "KEEP5", "memset", T.KEEP5[:, 0::5], 0.0)

    def unpack_hi(q):
        c0, c1, k = 512 * q, 512 * q + 512, str(q)
        V("PK%d" % (q // 2), "TI" + k, "ts", T.TI[:, c0:c1], T.PK[:, c0:c1], 12, None, AO.arith_shift_right)
        V("PFT TI" + k, "PFH" + k, "tc", T.PF[:, 2049 + c0:2049 + c1], T.TI[:, c0:c1])
        S("PFH" + k, "HP" + k, T["HP" + k][:], T.PF[:, 2049 + c0:2049 + c1], AF.Copy, scale=4096.0)

    def unpack_lo(q):
        c0, c1, k = 512 * q, 512 * q + 512, str(q)
        V("PFT PK%d HP%s" % (q // 2, k), "PFL" + k, "tt", T.PF[:, 1 + c0:1 + c1], T.PK[:, c0:c1], T["HP" + k][:], AO.subtract)
    PFA = "PFT " + " ".join("PFH%d PFL%d" % (q, q) for q in range(4))

    V("JI", "JF", "tc", T.JF[:, :, :], T.JI[:, :, :])
    for h in range(8):
        S("JF MG", "JT%d" % h, T.JT[:, :, 16 * h:16 * h + 16], T.JF[:, :, :], AF.Identity, scale=T.MG[:, h:h + 1])
    V("SRI", "SRB", "tc", T.SRB[0:8, :], T.SRI[0:8, :])
    mms("L8 SRB", "AUX0", [(T.AUX0[:, 0:256], T.L8[0:8, :], T.SRB[0:8, :], True, True)])
    V("", "PFT", "memset", T.PF[:, 0:16], 4096.0)
    V("", "PFT", "memset", T.PF[:, 4096:4112], 0.0)
    V("XRI", "XREP", "tc", T.XREP[:], T.XRI[:])
    V("AUX0", "SRG", "tc", T.SRG[:], T.AUX0[:, 0:256])
    mms("WB SRG", "AUX1", [(T.AUX1[:, 0:16], T.WB[:, 15 - b:143 - b], T.SRG[:, b::16], b == 0, b == 15) for b in range(16)])
    mms("JT0 JT1 JT2 JT3 JT4 JT5 JT6 JT7 E16", "KEY1", [(T.KEY1[:, 16 * a:16 * a + 16], T.JT[:, a, :], T.E16[:], True, True) for a in range(16)])
    V("KEEP", "KEEP", "memset", T.KEEP[:, 0::16], 0.0)
    V("RST", "RST", "memset", T.RST[:, 0::16], 67108864.0)
    V("IA CF1", "XL", "ts", T.XL[:], T.IA[:], q_c, None, AO.add)
    V("XL", "XLW", "ts", T.XLW[:, 0:8], T.XL[:, 0:8], 16.0, None, AO.mult)
    V("XL", "XLW", "ts", T.XLW[:, 8:16], T.XL[:, 0:8], 16.0, None, AO.mult)
    V("AUX1 XZ", "XZ", "ts", T.XZ[:, 0::16], T.AUX1[:, 0:16], 2.0 ** -21, None, AO.mult)
    V("AUX1", "ST0", "ts", T.ST0[:, 272:288], T.AUX1[:, 0:16], 2.0 ** -21, None, AO.mult)
    V("KEEP XZ", "XA", "scan", T.XA[:], T.KEEP[:, 0:256], T.XZ[:], 0.0, AO.mult, AO.add)
    V("XA QK", "XB", "tt", T.XB[:], T.XA[:], T.QK[:], AO.is_equal)
    unpack_hi(0)
    unpack_hi(1)
    V("KEY1 XB", "XC", "tt", T.XC[:], T.KEY1[:, 0:256], T.XB[:], AO.mult)
    V("KEY1 PLC", "ST0", "tt", T.ST0[:, 0:256], T.KEY1[:, 0:256], T.PLC[:], AO.add)
    V("KEEP XC", "XA", "scan", T.XA[:], T.KEEP[:, 0:256], T.XC[:], 0.0, AO.mult, AO.add)
    V("XA", "ST0", "ts", T.ST0[:, 256:272], T.XA[:, 15::16], 1.0, None, AO.add)
    send((rank + 1) % nrank, T.ST0[:], T.ST1[:], "aS1", "ST0")
    send((rank + 2) % nrank, T.ST0[:], T.ST2[:], "aS2", "ST0")
    Wr["ST1"], Wr["ST2"] = {"aS1": narr}, {"aS2": narr}
    Wr["FIN1"], Wr["FIN2"] = {"aF1": narr}, {"aF2": narr}

    def a5(buf, X, s):
        return buf[:, 40 * X + s:40 * X + 40:5]

    def opn(s):
        return T.OPN[:, s:80:5]

    def win(X):
        return T.WW[:, 4096 * X:4096 * X + 4096]

    def lists_of_visit(t):
        V("ST%d" % t, "LU01 LU11", "tc", T.LW[:, 8:24], T["ST%d" % t][:, 256:272])

    unpack_lo(0)
    unpack_hi(2)
    unpack_lo(1)
    unpack_hi(3)
    unpack_lo(2)
    lists_of_visit(0)
    unpack_lo(3)
    for t in range(3):
        st, stk = T["ST%d" % t], "ST%d" % t
        fin, fk = (T.FX0, "FX0") if t == 0 else (T["FIN%d" % t], "FIN%d" % t)
        fo, fok = T["FO%d" % t], "FO%d" % t

        def pf(X, s):
            c0, l0 = 256 * s - 256 + 128 * X, 32 * s - 24 + 8 * X
            V("%s LU%d%d" % (PFA, X, s), "NU%d%d" % (X, s), "tc", T.NU[:, c0:c0 + 128], T.PF[:, 0:4112].indirect(T.LW[:, l0:l0 + 8]))

        def pay(X):
            mms("IDN " + stk, "KEY%d" % X, [(T["KEY%d" % X][:, 0:128], T.IDN[:], st[:, 128 * X:128 * X + 128], True, False)])

        def fe(X, i):
            c0, c1 = 256 * FE[i][0], 256 * FE[i][1]
            if i == "v":
                V("KEEP FS%d" % X, "WF%dv" % X, "scan", T.WW[:, 4096 * X + c0:4096 * X + c1], T.KEEP[:, 0:c1 - c0],
                  T.FS[:, 2048 * X + c0:2048 * X + c1], 0.0, AO.mult, AO.add)
            else:
                S("XREP FS%d" % X, "WF%d%s" % (X, i), T.WW[:, 4096 * X + c0:4096 * X + c1],
                  T.FS[:, 2048 * X:2048 * X + 2048].indirect(T.XREP[:, c0 // 16:c1 // 16]), AF.Copy)

        def gather(X, i, s):
            c0, c1, n0 = 256 * CH[i][0], 256 * CH[i][1], 256 * s - 256 + 128 * X
            V("R %s NU%d%d" % ("WF%dv WF%da" % (X, X) if i == 0 else "WF%db" % X, X, s), "WD%d%d" % (X, i), "tt",
              T.WW[:, 4096 * X + 2048 + c0:4096 * X + 2048 + c1],
              T.R[:, 0:4096].indirect(T.NU[:, n0 + c0 // 16:n0 + c1 // 16]), T.WW[:, 4096 * X + c0:4096 * X + c1], AO.subtract)

        def dist(X, i):
            a0, a1 = CH[i]
            S("WD%d%d" % (X, i), "A%d%d" % (X, i), T.A3[:, 8 * X + a0:8 * X + a1, :], T.WW[:, 4096 * X + 2048 + 256 * a0:4096 * X + 2048 + 256 * a1], AF.Abs)
            mms("WB A%d%d" % (X, i), "KEY%d" % X, [(T["KEY%d" % X][:, 16 * a0:16 * a1], T.WB[:, 15 - b:143 - b],
                T.A3[:, 8 * X + a0:8 * X + a1, 16 * b:16 * b + 16], False, i == len(CH) - 1 and b == 15) for b in range(16)])

        def nh(s):
            S("%s LU0%d LU1%d" % (PFA, s, s), "NH%d" % s, T.NHF[:, 256 * s - 256:256 * s], T.PF[:, 0:4112].indirect(T.LW[:, 32 * s - 24:32 * s - 8]), AF.Copy)

        def choose(X, s, fill=(), last=()):
            k, c0, i0 = "%d%d" % (X, s), 256 * s - 256 + 128 * X, 32 * s - 32
            fa, cc = (i0, i0 + 8) if X == 0 else (i0 + 24, i0 + 16)
            key, fill, last = T.SC[:, c0 + 15:c0 + 128:16], list(fill), list(last)

            def some(n):
                while len(fill) > n:
                    fill.pop(0)()
            V("RST KEY%d" % X, "SC" + k, "scan", T.SC[:, c0:c0 + 128], T.RST[:], T["KEY%d" % X][:, 0:128], 0.0, AO.add, AO.min)
            mixed = len(fill) >= 3
            some(3 if len(fill) > 3 else 2 if mixed else 0)
            V("SC" + k, "HK" + k, "ts", a5(T.HK, X, s), key, 13, 15, AO.arith_shift_right, AO.bitwise_and)
            some(2)
            if s < 4:
                V("SC" + k, "CC" + k, "ts", T.CI[:, cc:cc + 8], key, 8191, None, AO.bitwise_and)
            some(1)
            for f in last[:1]:
                f()
            if mixed:
                if s < 4:
                    V("CC" + k, "LU%d%d" % (X, s + 1), "tc", T.LW[:, 32 + cc:40 + cc], T.CI[:, cc:cc + 8])
                some(0)
                if s < 4:
                    pf(X, s + 1)
            V("OX HK" + k, "FA" + k, "tt", T.CI[:, fa:fa + 8], a5(T.HK, X, s), T.OX[:, 8 * X:8 * X + 8], AO.add)
            if s < 4 and not mixed:
                V("CC" + k, "LU%d%d" % (X, s + 1), "tc", T.LW[:, 32 + cc:40 + cc], T.CI[:, cc:cc + 8])
            for f in last[1:]:
                f()
            V("FA" + k, "FL%d" % X, "tc", T.LW[:, 32 + fa:40 + fa], T.CI[:, fa:fa + 8])
            rd, fl = "FL%d WF%dv WF%da WF%db WD%d0 WD%d1" % (X, X, X, X, X, X), T.LW[:, 32 + fa:40 + fa]
            if s < 4:
                S(rd, "FS%d" % X, T.FS[:, 2048 * X:2048 * X + 2048:16], win(X).indirect(fl), AF.Abs)
                if not mixed:
                    pf(X, s + 1)
                pay(X)
            else:
                S(rd, fok, fo[:, 128 * X:128 * X + 128], win(X).indirect(fl), AF.Abs)

        def keep(s):
            H = [T.HK[:, j:80:5] for j in range(5)]
            hk = ["HK0%d HK1%d" % (j, j) for j in range(5)]
            todo = []

            def later(*a):
                todo.append(lambda: V(*a))

            def ne(j, out, key):
                later(hk[s] + " " + hk[j], key, "tt", out, H[s], H[j], AO.not_equal)

            def mul(out, x, y, ko, kx, ky):
                later(kx + " " + ky, ko, "tt", out, x, y, AO.mult)
            t0, t1, t2, t3 = T.T0[:], T.T1[:], T.T2[:], T.T3[:]
            if s == 1:
                ne(0, opn(1), "OPN1")
            else:
                for j in range(s):
                    ne(j, T["T%d" % j][:], "T%d" % j)
                if s == 2:
                    mul(t0, t0, opn(1), "T0", "T0", "OPN1")
                    mul(opn(2), t0, t1, "OPN2", "T0", "T1")
                elif s == 3:
                    mul(t0, t0, t1, "T0", "T0", "T1")
                    mul(t2, t2, opn(2), "T2", "T2", "OPN2")
                    mul(opn(3), t0, t2, "OPN3", "T0", "T2")
                else:
                    mul(t0, t0, t1, "T0", "T0", "T1")
                    mul(t2, t2, t3, "T2", "T2", "T3")
                    mul(t0, t0, opn(3), "T0", "T0", "OPN3")
                    mul(opn(4), t0, t2, "OPN4", "T0", "T2")
            if s < 4:
                later("OPN%d" % s, "OXT", "ts", T.OXT[:], opn(s), 2048.0, None, AO.mult)
                later("OXT XLW", "OX", "tt", T.OX[:], T.OXT[:], T.XLW[:], AO.add)
                later("CC0%d CC1%d OPN%d" % (s, s, s), "LST%d" % (s + 1), "tt", T.LST[:, 16 * s:16 * s + 16], T.CI[:, 32 * s - 24:32 * s - 8], opn(s), AO.mult)
            later("SC0%d SC1%d" % (s, s), "DP%d" % s, "ts", T.DP[:, s:80:5], T.SC[:, 256 * s - 241:256 * s:16], 17, 1, AO.arith_shift_right, AO.bitwise_and)
            return todo

        pay(0)
        pay(1)
        for X in range(2):
            S(fk, "FS%d" % X, T.FS[:, 2048 * X:2048 * X + 2048:16], fin[:, 128 * X:128 * X + 128], AF.Copy)
        mms("WB " + fk, "AUX1", [(T.AUX1[:, 0:16], T.WB[:, 15 - b:143 - b], fin[:, b::16], b == 0, b == 15) for b in range(16)])
        fe(0, "a")
        fe(0, "b")
        fe(1, "a")
        spare = []
        for s in range(1, 5):
            for X in range(2):
                fe(X, "v")
                if s == 1 and X == 0:
                    pf(0, 1)
                    pf(1, 1)
                elif s == 1:
                    V(stk, "LST1", "tc", T.LST[:, 0:16], st[:, 256:272])
                elif spare:
                    spare.pop()()
                gather(X, 0, s)
                dist(X, 0)
                if X == 1 and s < 4:
                    k2 = keep(s - 1) if s > 1 else []
                    choose(0, s, k2[:-2])
                    spare.extend(k2[-2:])
                    fe(0, "a")
                elif X == 0 and s > 1:
                    choose(1, s - 1)
                    fe(1, "a")
                gather(X, 1, s)
                dist(X, 1)
                if X == 0 or s < 4:
                    fe(1 - X, "b")
                if X == 0 and s == 1:
                    V("AUX1", "KF", "tc", T.KF[:], T.AUX1[:, 0:16])
                    V("HK " + stk, "HK00 HK10", "tc", T.HK[:, 0:80:5], st[:, 272:288])
                    V("XLW", "OX", "ts", T.OX[:], T.XLW[:], 2048.0, None, AO.add)
                    V("KF", "DP0", "ts", T.DP[:, 0:80:5], T.KF[:], 17, 1, AO.arith_shift_right, AO.bitwise_and)
                if X == 1:
                    nh(s)
        k3 = keep(3)
        choose(0, 4, k3[:-2])
        if t == 0:
            late_constants()
        for f in spare + k3[-2:]:
            f()
        LSA = "LST1 LST2 LST3 LST4"
        choose(1, 4, [lambda: V(LSA, "Q0", "ts", T.Q0[:], T.LST[:], 0.0, None, AO.is_equal)],
               [lambda: V("Q0 TR", "Q1", "tt", T.Q1[:], T.Q0[:], T.TR[:], AO.mult),
                lambda: V("Q1 " + LSA, "Q2", "tt", T.Q2[:], T.Q1[:], T.LST[:], AO.add)])
        if t < 2:
            send((rank + 1) % nrank, fo[:], T["FIN%d" % (t + 1)][:], "aF%d" % (t + 1), fok)
        else:
            dma("Y", fok, "yf", T.yf[:], fo[:])
        HKA = "HK " + " ".join("HK%d%d" % (X, s) for X in range(2) for s in range(5))
        OPA, NHA = "OPN OPN1 OPN2 OPN3 OPN4", "NH1 NH2 NH3 NH4"
        Q = [T.QB[:, 80 * i:80 * i + 80] for i in range(5)]
        k4 = keep(4)
        for f in k4[:6]:
            f()
        V("Q2", "SL", "tc", T.SL[:], T.Q2[:])
        V(HKA, "H16", "ts", T.H16[:, 0:81], T.HK[:, 0:81], 16.0, None, AO.add)
        k4[6]()
        k4[8]()
        if t < 2:
            lists_of_visit(t + 1)
        k4[7]()
        V("DP0 DP1 DP2 DP3 DP4 AS", "AS", "tt", T.AS[:, 0:79], T.DP[:, 0:79], T.DP[:, 1:80], AO.add)
        V(OPA, "CLB", "tt", T.CLB[:], T.OPN[:, 0:80], T.OPN[:, 1:81], AO.subtract)
        if t > 0:
            V("AS ZA", "AS", "ts", T.AS[:], T.AS[:], T.ZA[:, 0:1], None, AO.add)
        V("CLB H16", "QB3", "tt", Q[3], T.CLB[:], T.H16[:, 1:81], AO.mult)
        V("CLB SI", "QB2", "tt", Q[2], T.CLB[:], T.SI[:], AO.mult)
        V("KEEP5 QB3", "KSS", "scan", T.KSS[:], T.KEEP5[:, 0:80], Q[3], 0.0, AO.mult, AO.add)
        V("AS", "OD", "ts", T.OD[:], T.AS[:], 1, None, AO.bitwise_and)
        for j in range(4):
            V("H16 KSS EQB", "EQ%d" % j, "tt", T.EQB[:, j::5], T.H16[:, j:80:5], T.KSS[:, 3::5], AO.is_equal)
        if t < 2:
            V(OPA, "ZR", "red", T.ZR[:, 0:1], T.OPN[:, 4:80:5], AxisListType.X, AO.add)
        V("EQB EQ0 EQ1 EQ2 EQ3 " + OPA, "GB", "tt", T.GB[:], T.EQB[:], T.OPN[:, 0:80], AO.mult)
        V("GB SI", "QB0", "tt", Q[0], T.GB[:], T.SI[:], AO.mult)
        V("GB H16", "QB1", "tt", Q[1], T.GB[:], T.H16[:, 1:81], AO.mult)
        V("GB OD", "QB4", "tt", Q[4], T.GB[:], T.OD[:], AO.mult)
        V("KEEP5 GB", "PG", "scan", T.PG[:], T.KEEP5[:, 0:80], T.GB[:], 0.0, AO.mult, AO.add)
        V("KEEP5 QB0 QB1 QB2 QB3 QB4", "QS", "scan", T.QS[:], T.KEEP5[:], T.QB[:], 0.0, AO.mult, AO.add)
        V("PG " + OPA, "UB", "tt", T.UB[:], T.PG[:], T.OPN[:, 0:80], AO.mult)
        V("QS", "DF", "tt", T.DF[:], T.QS[:, 163:320:5], T.QS[:, 3:160:5], AO.subtract)
        V("UB H16", "KU", "tt", T.KU[:], T.UB[:], T.H16[:, 1:81], AO.mult)
        V("DF QS", "DG1", "tt", T.DG[:, 16:32], T.DF[:, 16:32], T.QS[:, 323:400:5], AO.mult)
        V("DF QS", "DG0", "tt", T.DG[:, 0:16], T.DF[:, 0:16], T.QS[:, 323:400:5], AO.mult)
        V("KU", "LC0", "tc", T.LC[:, 0:16], T.KU[:, 0::5])
        V("DG0 DG1 QS", "RS", "tt", T.RS[:], T.DG[:], T.QS[:, 3:160:5], AO.add)
        V("KU", "LC1", "tc", T.LC[:, 16:32], T.KU[:, 1::5])
        V("RS", "LKD", "tc", T.LKD[:], T.RS[:, 16:32])
        V("RS XL", "LJA", "tt", T.LJA[:], T.RS[:, 0:16], T.XL[:], AO.add)
        S("OHW LKD", "OHD", T.OHD[:], T.OHW[:, 0:32].indirect(T.LKD[:, 0:16]), AF.Copy)
        V("KU", "LC2", "tc", T.LC[:, 32:48], T.KU[:, 2::5])
        V("LJA", "LJD", "tc", T.LJD[:], T.LJA[:])
        V("KU", "LC3", "tc", T.LC[:, 48:64], T.KU[:, 3::5])
        S("OHW LC0 LC1 LC2 LC3", "OHM", T.OHM[:], T.OHW[:, 0:32].indirect(T.LC[:, 0:64]), AF.Copy)
        V("OHD LJD " + NHA, "SEL", "tt", T.SEL[:], T.NHF[:, 0:1024].indirect(T.LJD[:, 0:16]), T.OHD[:], AO.mult)
        mms("BO SEL", "AUX0", [(T.AUX0[:, 0:256], T.BO[:], T.SEL[:], True, True)])
        if t < 2:
            mms("ONE ZR", "AUX1", [(T.AUX1[:, 0:1], T.ONE[:], T.ZR[:, 0:1], True, True)])
        V("OHC LC0 LC1 LC2 LC3 " + NHA, "NP", "tt", T.NP[:], T.OHC[:, 0:32].indirect(T.LC[:, 0:64]), T.NHF[:], AO.mult)
        for s in range(4):
            V("AUX0 OHM", "BB%d" % s, "tt", T.BB[:, 256 * s:256 * s + 256], T.AUX0[:, 0:256], T.OHM[:, 256 * s:256 * s + 256], AO.mult)
        if t == 0:
            V("AUX1", "ZA", "tc", T.ZA[:, 0:1], T.AUX1[:, 0:1])
        elif t == 1:
            V("AUX1 ZA", "ZA", "tt", T.ZA[:, 0:1], T.AUX1[:, 0:1], T.ZA[:, 0:1], AO.add)
        V("NP BB0 BB1 BB2 BB3 SL", PFA, "tt", T.PF[:, 0:5136].indirect(T.SL[:, 0:64]), T.NP[:], T.BB[:], AO.add)
    for q in range(4):
        c0, c1, k = 512 * q, 512 * q + 512, str(q)
        S("PFH" + k, "HP" + k, T["HP" + k][:], T.PF[:, 2049 + c0:2049 + c1], AF.Copy, scale=4096.0)
        V("HP%s PFL%s" % (k, k), "YO" + k, "tt", T.YO[:, c0:c1], T["HP" + k][:], T.PF[:, 1 + c0:1 + c1], AO.add)
        dma("Y", "YO" + k, "yp", T.yp[:, c0:c1], T.YO[:, c0:c1])
    for sem in SEMAPHORES:
        if cnt[sem] and sem != "ls":
            need("G", sem, cnt[sem])
    need("G", "ls", cnt["ls"])
    for sem in ("aS1", "aS2", "aF1", "aF2"):
        need("G", sem, narr)
